import numpy as np
import ml_dtypes


def mxq(x, axis, fmt="e4m3"):
    dtype, down = {"e4m3": (ml_dtypes.float8_e4m3fn, 7), "e5m2": (ml_dtypes.float8_e5m2, 14)}[fmt]
    v = np.moveaxis(np.asarray(x, np.float32).astype(ml_dtypes.bfloat16).astype(np.float64), axis, -1)
    blocks = v.reshape(v.shape[:-1] + (-1, 32))
    amax = np.abs(blocks).max(-1, keepdims=True)
    byte = np.maximum(np.where(amax > 0, np.frexp(amax)[1] - 1 + 127, 0) - down, 1)
    scale = np.exp2(byte - 127.0)
    codes = (blocks / scale).astype(np.float32).astype(dtype).astype(np.float64)
    return np.moveaxis((codes * scale).reshape(v.shape), -1, axis)


WIDE = False


def mx_kscale(k):
    if not WIDE:
        return np.ones(k)
    levels = np.array([10, -10, 5, -5, 0])
    if k % 512:
        return np.exp2(np.random.permutation(np.resize(levels, k // 32))).repeat(32)
    a = np.empty((k // 512, 16))
    for p in range(k // 512):
        a[p, :8] = np.random.permutation(np.resize(levels, 8))
        for g in range(8):
            far = levels[np.abs(levels - a[p, g]) >= 10]
            a[p, g + 8] = far[np.random.randint(len(far))]
    return np.exp2(a.ravel()).repeat(32)


def f64(x):
    return np.asarray(x).astype(np.float64)


def striped(idx):
    return np.tile(idx.reshape(-1, 16).T, (8, 1)).astype(np.uint16)


def unstriped(offs):
    return offs[:16].T.reshape(-1).astype(np.int64)


def striped8(idx):
    return np.concatenate([x.reshape(-1, 16).T for x in idx]).astype(np.uint16)


def runs(offs, k):
    lists = np.stack([offs[16 * r : 16 * r + 16].T.reshape(-1) for r in range(8)]).astype(np.int64)
    return lists[np.arange(k) % 512 // 64]


def pack_weight(w):
    k, n = w.shape
    w = f64(np.asarray(w, np.float32).astype(ml_dtypes.bfloat16)).reshape(k // 32, 32, n)
    amax = np.abs(w).max(1)
    byte = np.clip(np.where(amax > 0, np.frexp(amax)[1] - 1 + 127 - 7, 1), 1, 254)
    scaled = (w * np.exp2(127.0 - byte)[:, None, :]).reshape(k, n).astype(np.float32)
    words = np.ascontiguousarray(scaled.reshape(k // 512, 128, 4, n).transpose(0, 1, 3, 2)).astype(ml_dtypes.float8_e4m3fn).view(np.uint8)
    return words, np.ascontiguousarray(byte.astype(np.uint8).reshape(k // 512, 16, n))


def unpack_weight(words, scales):
    g, p, n, _ = words.shape
    vals = np.ascontiguousarray(words).view(ml_dtypes.float8_e4m3fn).astype(np.float64) * np.repeat(np.exp2(scales.astype(np.float64) - 127.0), 8, axis=1)[..., None]
    return vals.transpose(0, 1, 3, 2).reshape(g * 512, n)

def planes(y):
    n, m = y.shape
    v = y.astype(np.float32).astype(ml_dtypes.bfloat16).astype(np.float64).reshape(n // 32, 32, m)
    top = np.abs(v).max(1)
    byte = np.clip(np.where(top > 0, np.frexp(top)[1] - 1 + 127 - 7, 1), 1, 254)
    codes = (v * np.exp2(127.0 - byte)[:, None, :]).reshape(n, m).astype(np.float32).astype(ml_dtypes.float8_e4m3fn).view(np.uint8)
    words = codes.reshape(n // 512, 128, 4, m).transpose(0, 1, 3, 2)
    return np.ascontiguousarray(words), np.ascontiguousarray(byte.astype(np.uint8).reshape(n // 512, 16, m))


K, T, S, V, N, H = 512, 2048, 512, 256, 512, 512


def setup_inputs():
    n = np.random.standard_normal
    s = mx_kscale(K)[:, None]
    u = mx_kscale(H)
    packed_xT = pack_weight(n((K, T)) * s)
    packed_w1 = pack_weight(n((K, H)) / np.sqrt(K) / s)
    packed_w2 = pack_weight(n((H, N)) / np.sqrt(H) / u[:, None])
    perm = np.stack([np.random.permutation(S) for _ in range(8)])
    return {
        "x_words": packed_xT[0],
        "x_scales": packed_xT[1],
        "w1_words": packed_w1[0],
        "w1_scales": packed_w1[1],
        "gn": (np.random.uniform(0.5, 1.5, (H, 1)) * u[:, None]).astype(np.float32),
        "w2_words": packed_w2[0],
        "w2_scales": packed_w2[1],
        "offs": striped(np.random.permutation(T)[:S]),
        "la": striped8(perm[:, :V]),
        "lb": striped8(perm[:, V:]),
    }


def reference(x_words, x_scales, w1_words, w1_scales, gn, w2_words, w2_scales, offs, la, lb):
    xq = unpack_weight(x_words, x_scales)[:, unstriped(offs)]
    y = unpack_weight(w1_words, w1_scales).T @ xq
    p = np.tanh(y[np.arange(H)[:, None], runs(la, H)])
    h = y.copy()
    h[np.arange(H)[:, None], runs(la, H)] = p
    q = h[np.arange(H)[:, None], runs(lb, H)] - (h[np.arange(H)[:, None], runs(la, H)])
    h2 = h.copy()
    h2[np.arange(H)[:, None], runs(lb, H)] = q
    z = f64(gn) * h2
    out_0 = unpack_weight(w2_words, w2_scales).T @ mxq(z, 0, "e4m3")
    return (out_0,) + planes(out_0)

@@ -1,0 +1,205 @@
+from contextlib import ExitStack
+
+import concourse.mybir as mybir
+
+K, T, S, V, H, N = 512, 2048, 512, 256, 512, 512
+FLOPS = 2 * K * H * S + 2 * H * N * S
+
+F32 = mybir.dt.float32
+BF16 = mybir.dt.bfloat16
+I32 = mybir.dt.int32
+U32 = mybir.dt.uint32
+U16 = mybir.dt.uint16
+U8 = mybir.dt.uint8
+FP8X4 = mybir.dt.float8_e4m3fn_x4
+ACT = mybir.ActivationFunctionType
+ALU = mybir.AluOpType
+
+P = 128
+PACK = 4
+CHUNK = 128
+CHUNKS = S // CHUNK
+PLANE_ORDER = (0, 2, 3, 1)
+
+
+def as_words(dram):
+    return dram[0].rearrange("p n t -> p (n t)").bitcast(I32)
+
+
+def load_scale_rows(queue, tile, dram):
+    rows = dram[0].bitcast(I32)
+    for q in range(4):
+        queue.dma_start(out=tile[32 * q : 32 * q + 4, :].bitcast(I32), in_=rows[4 * q : 4 * q + 4, :])
+
+
+def deal(nc, dealt, raw):
+    nc.vector.tensor_copy(out=dealt[:].rearrange("p (t m) -> p m t", t=PACK), in_=raw[:].rearrange("p (m t) -> p m t", t=PACK))
+
+
+def tile_picked_fixedpt_tanh_po_kernel(tc, x_words, x_scales, w1_words, w1_scales, gn, w2_words, w2_scales, offs, la, lb, out_0, out_1, out_2):
+    nc = tc.nc
+    with ExitStack() as ctx:
+        keep = ctx.enter_context(tc.tile_pool(name="keep", bufs=1))
+        ring = ctx.enter_context(tc.tile_pool(name="ring", bufs=3))
+        psum = ctx.enter_context(tc.psum_pool(name="psum", bufs=1))
+
+        offs_t = keep.tile([P, S // 16], U16, name="offs_t")
+        la_t = keep.tile([P, V // 16], U16, name="la_t")
+        lb_t = keep.tile([P, V // 16], U16, name="lb_t")
+        xw = keep.tile([P, T], I32, name="xw", align_bytes=64)
+        xs = keep.tile([P, T], U8, name="xs", align_bytes=64)
+        w1w_raw = keep.tile([P, H], I32, name="w1w_raw", align_bytes=64)
+        w1s_raw = keep.tile([P, H], U8, name="w1s_raw", align_bytes=64)
+        w2w_raw = keep.tile([P, N], I32, name="w2w_raw", align_bytes=64)
+        w2s_raw = keep.tile([P, N], U8, name="w2s_raw", align_bytes=64)
+        w1w = keep.tile([P, H], I32, name="w1w", align_bytes=64)
+        w1s = keep.tile([P, H], U8, name="w1s", align_bytes=64)
+        w2w = keep.tile([P, N], I32, name="w2w", align_bytes=64)
+        w2s = keep.tile([P, N], U8, name="w2s", align_bytes=64)
+        gain = keep.tile([P, PACK], F32, name="gain")
+        minus_one = keep.tile([P, V], F32, name="minus_one", align_bytes=64)
+        warm = keep.tile([P, 1], F32, name="warm")
+        xgw = keep.tile([P, S], I32, name="xgw", align_bytes=64)
+        xgs = keep.tile([P, S], U8, name="xgs", align_bytes=64)
+
+        nc.vector.memset(xs[:].bitcast(I32), 0)
+        nc.vector.memset(w1s_raw[:].bitcast(I32), 0)
+        nc.gpsimd.memset(minus_one[:], -1.0)
+        nc.gpsimd.memset(w2s_raw[:].bitcast(I32), 0)
+
+        nc.sync.dma_start(offs_t[:], offs)
+        nc.sync.dma_start(out=w1w_raw[:], in_=as_words(w1_words))
+        load_scale_rows(nc.scalar, xs, x_scales)
+        nc.sync.dma_start(out=xw[:], in_=as_words(x_words))
+        load_scale_rows(nc.scalar, w1s_raw, w1_scales)
+        nc.scalar.activation(warm[:], minus_one[:, 0:1], ACT.Tanh)
+        nc.sync.dma_start(out=w2w_raw[:], in_=as_words(w2_words))
+        nc.sync.dma_start(la_t[:], la)
+        nc.sync.dma_start(lb_t[:], lb)
+        load_scale_rows(nc.sync, w2s_raw, w2_scales)
+        nc.sync.dma_start(out=gain[:], in_=gn.rearrange("(p t) o -> p (t o)", t=PACK))
+
+        deal(nc, w1w, w1w_raw)
+        nc.vector.tensor_copy(xgs[:], xs[:].indirect(offs_t[:]))
+        deal(nc, w1s, w1s_raw)
+        HALF = S // 2
+        for u in range(2):
+            nc.vector.tensor_copy(xgw[:, u * HALF : (u + 1) * HALF].bitcast(U32),
+                                  xw[:].bitcast(U32).indirect(offs_t[:, u * HALF // 16 : (u + 1) * HALF // 16]))
+        deal(nc, w2w, w2w_raw)
+        deal(nc, w2s, w2s_raw)
+
+        y_ps = {}
+        for t in PLANE_ORDER:
+            cols = slice(t * P, (t + 1) * P)
+            parts = [slice(0, HALF), slice(HALF, S)] if t == PLANE_ORDER[0] else [slice(0, S)]
+            y_ps[t] = []
+            for u, part in enumerate(parts):
+                bank = psum.tile([P, part.stop - part.start], F32, name="y_ps%d_%d" % (t, u))
+                nc.tensor.matmul_mx(out=bank[:], lhsT=w1w[:, cols].bitcast(FP8X4), lhsT_scale=w1s[:, cols],
+                                    rhs=xgw[:, part].bitcast(FP8X4), rhs_scale=xgs[:, part], start=True, stop=True)
+                y_ps[t].append((part, bank))
+
+        zb = [keep.tile([P, CHUNK, PACK], BF16, name="zb%d" % c, align_bytes=64) for c in range(CHUNKS)]
+        neg_tanh, state, neg_p, y_b = {}, {}, {}, {}
+
+        def leave_tanh(t):
+            neg_tanh[t] = keep.tile([P, S], F32, name="neg_tanh%d" % t, align_bytes=64)
+            for part, bank in y_ps[t]:
+                nc.scalar.activation(neg_tanh[t][:, part], bank[:], ACT.Tanh, scale=-1.0)
+
+        def leave_state(t):
+            state[t] = ring.tile([P, S], F32, name="state", align_bytes=64)
+            for part, bank in y_ps[t]:
+                nc.scalar.copy(state[t][:, part], bank[:])
+
+        def gather_a(t):
+            neg_p[t] = keep.tile([P, V], F32, name="neg_p%d" % t, align_bytes=64)
+            nc.vector.tensor_copy(neg_p[t][:], neg_tanh[t][:].indirect(la_t[:]))
+
+        def gather_b(t):
+            y_b[t] = keep.tile([P, V], F32, name="y_b%d" % t, align_bytes=64)
+            nc.vector.tensor_copy(y_b[t][:], state[t][:].indirect(lb_t[:]))
+
+        def scatter_a(t):
+            nc.vector.tensor_tensor(state[t][:].indirect(la_t[:]), neg_p[t][:], minus_one[:], ALU.mult)
+
+        def scatter_b(t):
+            nc.vector.tensor_tensor(state[t][:].indirect(lb_t[:]), y_b[t][:], neg_p[t][:], ALU.add)
+
+        def round_scalar(t, c):
+            nc.scalar.activation(zb[c][:, :, t], state[t][:, c * CHUNK : (c + 1) * CHUNK], ACT.Copy, scale=gain[:, t : t + 1])
+
+        def round_vector(t, c):
+            nc.vector.tensor_scalar(zb[c][:, :, t], state[t][:, c * CHUNK : (c + 1) * CHUNK], gain[:, t : t + 1], None, ALU.mult)
+
+        a, b, c3, d = PLANE_ORDER
+        for t in (a, b, c3):
+            leave_tanh(t)
+            leave_state(t)
+        leave_tanh(d)
+        gather_a(a)
+        gather_b(a)
+        gather_a(b)
+        scatter_a(a)
+        gather_b(b)
+        scatter_b(a)
+        for c in range(CHUNKS):
+            round_scalar(a, c)
+        leave_state(d)
+        gather_a(c3)
+        scatter_a(b)
+        gather_b(c3)
+        scatter_b(b)
+        for c in range(CHUNKS):
+            round_scalar(b, c)
+        gather_a(d)
+        gather_b(d)
+        scatter_a(c3)
+        scatter_a(d)
+        scatter_b(c3)
+        for c in range(CHUNKS):
+            round_scalar(c3, c)
+        scatter_b(d)
+        round_vector(d, 0)
+        round_vector(d, 1)
+        round_scalar(d, 2)
+        round_scalar(d, 3)
+
+        zw = keep.tile([P, S], I32, name="zw", align_bytes=64)
+        zs = keep.tile([P, S], U8, name="zs", align_bytes=64)
+        ow = keep.tile([P, S], I32, name="ow", align_bytes=64)
+        osc = keep.tile([P, S], U8, name="osc", align_bytes=64)
+        out_rows = out_0.rearrange("(p t) j -> p t j", t=PACK)
+        out_words = as_words(out_1)
+        res = []
+        for c in range(CHUNKS):
+            cols = slice(c * CHUNK, (c + 1) * CHUNK)
+            nc.vector.quantize_mx(out=zw[:, cols].bitcast(FP8X4), scales=zs[:, cols], in_=zb[c][:].rearrange("p j t -> p (j t)"))
+        for c in range(CHUNKS):
+            cols = slice(c * CHUNK, (c + 1) * CHUNK)
+            o_ps = psum.tile([P, PACK, CHUNK], F32, name="o_ps%d" % c if c < CHUNKS - 1 else "y_ps0_0")
+            for t in range(PACK):
+                m = slice(t * P, (t + 1) * P)
+                nc.tensor.matmul_mx(out=o_ps[:, t, :], lhsT=w2w[:, m].bitcast(FP8X4), lhsT_scale=w2s[:, m],
+                                    rhs=zw[:, cols].bitcast(FP8X4), rhs_scale=zs[:, cols], start=True, stop=True)
+            o_sb = keep.tile([P, PACK, CHUNK], F32, name="o_sb%d" % c, align_bytes=64)
+            nc.scalar.copy(o_sb[:], o_ps[:])
+            nc.sync.dma_start(out=out_rows[:, :, cols], in_=o_sb[:])
+            res.append(o_sb)
+        ob = []
+        for c in range(CHUNKS + 1):
+            if c < CHUNKS:
+                o_bf = keep.tile([P, CHUNK, PACK], BF16, name="o_bf%d" % c, align_bytes=64)
+                nc.vector.tensor_copy(out=o_bf[:].rearrange("p (g i) t -> p g t i", i=4), in_=res[c][:].rearrange("p t (g i) -> p g t i", i=4))
+                ob.append(o_bf)
+            if c > 0:
+                cols = slice((c - 1) * CHUNK, c * CHUNK)
+                nc.vector.quantize_mx(out=ow[:, cols].bitcast(FP8X4), scales=osc[:, cols], in_=ob[c - 1][:].rearrange("p j t -> p (j t)"))
+                if c % 2 == 0:
+                    half = slice((c - 2) * CHUNK, c * CHUNK)
+                    nc.sync.dma_start(out=out_words[:, half], in_=ow[:, half])
+        scale_rows = out_2[0].bitcast(I32)
+        for q in range(4):
+            queue = nc.sync if q % 2 == 0 else nc.scalar
+            queue.dma_start(out=scale_rows[4 * q : 4 * q + 4, :], in_=osc[32 * q : 32 * q + 4, :].bitcast(I32))

@@ -26,9 +26,9 @@ def as_words(dram):
     return dram[0].rearrange("p n t -> p (n t)").bitcast(I32)
 
 
-def load_scale_rows(queue, tile, dram):
+def load_scale_rows(queues, tile, dram):
     rows = dram[0].bitcast(I32)
-    for q in range(4):
+    for q, queue in enumerate(queues):
         queue.dma_start(out=tile[32 * q : 32 * q + 4, :].bitcast(I32), in_=rows[4 * q : 4 * q + 4, :])
 
 
@@ -46,47 +46,52 @@ def tile_picked_fixedpt_tanh_po_kernel(tc, x_words, x_scales, w1_words, w1_scale
         offs_t = keep.tile([P, S // 16], U16, name="offs_t")
         la_t = keep.tile([P, V // 16], U16, name="la_t")
         lb_t = keep.tile([P, V // 16], U16, name="lb_t")
-        xw = keep.tile([P, T], I32, name="xw", align_bytes=64)
-        xs = keep.tile([P, T], U8, name="xs", align_bytes=64)
-        w1w_raw = keep.tile([P, H], I32, name="w1w_raw", align_bytes=64)
-        w1s_raw = keep.tile([P, H], U8, name="w1s_raw", align_bytes=64)
-        w2w_raw = keep.tile([P, N], I32, name="w2w_raw", align_bytes=64)
-        w2s_raw = keep.tile([P, N], U8, name="w2s_raw", align_bytes=64)
+        xw = keep.tile([P, T], I32, name="xw", tag="xw_slot", align_bytes=64)
+        xs = keep.tile([P, T], U8, name="xs", tag="xs_slot", align_bytes=64)
+        w1w_raw = keep.tile([P, H], I32, name="w1w_raw", tag="w1w_slot", align_bytes=64)
+        w1s_raw = keep.tile([P, H], U8, name="w1s_raw", tag="w1s_slot", align_bytes=64)
         w1w = keep.tile([P, H], I32, name="w1w", align_bytes=64)
-        w1s = keep.tile([P, H], U8, name="w1s", align_bytes=64)
+        w1s_first = keep.tile([P, P], U8, name="w1s_first", align_bytes=64)
         w2w = keep.tile([P, N], I32, name="w2w", align_bytes=64)
-        w2s = keep.tile([P, N], U8, name="w2s", align_bytes=64)
-        gain = keep.tile([P, PACK], F32, name="gain")
         minus_one = keep.tile([P, V], F32, name="minus_one", align_bytes=64)
         warm = keep.tile([P, 1], F32, name="warm")
-        xgw = keep.tile([P, S], I32, name="xgw", align_bytes=64)
         xgs = keep.tile([P, S], U8, name="xgs", align_bytes=64)
+        xgw = keep.tile([P, S], I32, name="xgw", align_bytes=64)
 
-        nc.vector.memset(xs[:].bitcast(I32), 0)
-        nc.vector.memset(w1s_raw[:].bitcast(I32), 0)
-        nc.gpsimd.memset(minus_one[:], -1.0)
-        nc.gpsimd.memset(w2s_raw[:].bitcast(I32), 0)
+        SPLIT = 288
+        nc.vector.memset(xs[:].bitcast(I32)[:, :SPLIT], 0)
+        nc.gpsimd.memset(xs[:].bitcast(I32)[:, SPLIT:], 0)
+        nc.vector.memset(minus_one[:], -1.0)
+        nc.gpsimd.memset(w1s_raw[:].bitcast(I32), 0)
 
         nc.sync.dma_start(offs_t[:], offs)
         nc.sync.dma_start(out=w1w_raw[:], in_=as_words(w1_words))
-        load_scale_rows(nc.scalar, xs, x_scales)
-        nc.sync.dma_start(out=xw[:], in_=as_words(x_words))
-        load_scale_rows(nc.scalar, w1s_raw, w1_scales)
-        nc.scalar.activation(warm[:], minus_one[:, 0:1], ACT.Tanh)
-        nc.sync.dma_start(out=w2w_raw[:], in_=as_words(w2_words))
         nc.sync.dma_start(la_t[:], la)
+        load_scale_rows([nc.scalar, nc.scalar, nc.sync, nc.sync], xs, x_scales)
+        nc.sync.dma_start(out=xw[:], in_=as_words(x_words))
+        load_scale_rows([nc.sync] * 4, w1s_raw, w1_scales)
         nc.sync.dma_start(lb_t[:], lb)
-        load_scale_rows(nc.sync, w2s_raw, w2_scales)
-        nc.sync.dma_start(out=gain[:], in_=gn.rearrange("(p t) o -> p (t o)", t=PACK))
+        nc.scalar.activation(warm[:], minus_one[:, 0:1], ACT.Tanh)
 
         deal(nc, w1w, w1w_raw)
+        w2s_raw = keep.tile([P, N], U8, name="w2s_raw", tag="w1w_slot", align_bytes=64)
+        nc.gpsimd.memset(w2s_raw[:].bitcast(I32), 0)
+        load_scale_rows([nc.scalar] * 4, w2s_raw, w2_scales)
         nc.vector.tensor_copy(xgs[:], xs[:].indirect(offs_t[:]))
-        deal(nc, w1s, w1s_raw)
+        w2w_raw = keep.tile([P, N], I32, name="w2w_raw", tag="xs_slot", align_bytes=64)
+        nc.sync.dma_start(out=w2w_raw[:], in_=as_words(w2_words))
         HALF = S // 2
+        w1s_by_plane = w1s_raw[:].rearrange("p (m t) -> p m t", t=PACK)
+        nc.vector.tensor_copy(out=w1s_first[:], in_=w1s_by_plane[:, :, 0])
         for u in range(2):
             nc.vector.tensor_copy(xgw[:, u * HALF : (u + 1) * HALF].bitcast(U32),
                                   xw[:].bitcast(U32).indirect(offs_t[:, u * HALF // 16 : (u + 1) * HALF // 16]))
+        w1s_rest = keep.tile([P, (PACK - 1) * P], U8, name="w1s_rest", tag="xw_slot", align_bytes=64)
+        nc.vector.tensor_copy(out=w1s_rest[:].rearrange("p (t m) -> p m t", t=PACK - 1), in_=w1s_by_plane[:, :, 1:])
+        gain = keep.tile([P, PACK], F32, name="gain", tag="w1s_slot", align_bytes=64)
+        nc.sync.dma_start(out=gain[:], in_=gn.rearrange("(p t) o -> p (t o)", t=PACK))
         deal(nc, w2w, w2w_raw)
+        w2s = keep.tile([P, N], U8, name="w2s", tag="xs_slot", align_bytes=64)
         deal(nc, w2s, w2s_raw)
 
         y_ps = {}
@@ -96,7 +101,7 @@ def tile_picked_fixedpt_tanh_po_kernel(tc, x_words, x_scales, w1_words, w1_scale
             y_ps[t] = []
             for u, part in enumerate(parts):
                 bank = psum.tile([P, part.stop - part.start], F32, name="y_ps%d_%d" % (t, u))
-                nc.tensor.matmul_mx(out=bank[:], lhsT=w1w[:, cols].bitcast(FP8X4), lhsT_scale=w1s[:, cols],
+                nc.tensor.matmul_mx(out=bank[:], lhsT=w1w[:, cols].bitcast(FP8X4), lhsT_scale=w1s_first[:] if t == 0 else w1s_rest[:, (t - 1) * P : t * P],
                                     rhs=xgw[:, part].bitcast(FP8X4), rhs_scale=xgs[:, part], start=True, stop=True)
                 y_ps[t].append((part, bank))
 
@@ -176,30 +181,38 @@ def tile_picked_fixedpt_tanh_po_kernel(tc, x_words, x_scales, w1_words, w1_scale
         for c in range(CHUNKS):
             cols = slice(c * CHUNK, (c + 1) * CHUNK)
             nc.vector.quantize_mx(out=zw[:, cols].bitcast(FP8X4), scales=zs[:, cols], in_=zb[c][:].rearrange("p j t -> p (j t)"))
+        spare = ["y_ps0_0", "y_ps0_1"]
         for c in range(CHUNKS):
             cols = slice(c * CHUNK, (c + 1) * CHUNK)
-            o_ps = psum.tile([P, PACK, CHUNK], F32, name="o_ps%d" % c if c < CHUNKS - 1 else "y_ps0_0")
-            for t in range(PACK):
-                m = slice(t * P, (t + 1) * P)
-                nc.tensor.matmul_mx(out=o_ps[:, t, :], lhsT=w2w[:, m].bitcast(FP8X4), lhsT_scale=w2s[:, m],
-                                    rhs=zw[:, cols].bitcast(FP8X4), rhs_scale=zs[:, cols], start=True, stop=True)
+            groups = [range(PACK)] if c < CHUNKS - 1 else [range(0, 2), range(2, PACK)]
             o_sb = keep.tile([P, PACK, CHUNK], F32, name="o_sb%d" % c, align_bytes=64)
-            nc.scalar.copy(o_sb[:], o_ps[:])
+            for g, planes in enumerate(groups):
+                o_ps = psum.tile([P, len(planes), CHUNK], F32, name="o_ps%d" % c if c < CHUNKS - 1 else spare[g])
+                for t in planes:
+                    m = slice(t * P, (t + 1) * P)
+                    nc.tensor.matmul_mx(out=o_ps[:, t - planes.start, :], lhsT=w2w[:, m].bitcast(FP8X4), lhsT_scale=w2s[:, m],
+                                        rhs=zw[:, cols].bitcast(FP8X4), rhs_scale=zs[:, cols], start=True, stop=True)
+                if c == 1:
+                    nc.vector.tensor_copy(o_sb[:, planes.start : planes.stop, :], o_ps[:])
+                else:
+                    nc.scalar.copy(o_sb[:, planes.start : planes.stop, :], o_ps[:])
             nc.sync.dma_start(out=out_rows[:, :, cols], in_=o_sb[:])
-            res.append(o_sb)
+            res.append((o_sb, groups))
         ob = []
         for c in range(CHUNKS + 1):
             if c < CHUNKS:
                 o_bf = keep.tile([P, CHUNK, PACK], BF16, name="o_bf%d" % c, align_bytes=64)
-                nc.vector.tensor_copy(out=o_bf[:].rearrange("p (g i) t -> p g t i", i=4), in_=res[c][:].rearrange("p t (g i) -> p g t i", i=4))
+                o_sb, groups = res[c]
+                for planes in groups:
+                    part = slice(planes.start, planes.stop)
+                    nc.vector.tensor_copy(out=o_bf[:, :, part].rearrange("p (g i) t -> p g t i", i=4),
+                                          in_=o_sb[:, part, :].rearrange("p t (g i) -> p g t i", i=4))
                 ob.append(o_bf)
             if c > 0:
                 cols = slice((c - 1) * CHUNK, c * CHUNK)
                 nc.vector.quantize_mx(out=ow[:, cols].bitcast(FP8X4), scales=osc[:, cols], in_=ob[c - 1][:].rearrange("p j t -> p (j t)"))
-                if c % 2 == 0:
-                    half = slice((c - 2) * CHUNK, c * CHUNK)
-                    nc.sync.dma_start(out=out_words[:, half], in_=ow[:, half])
+        nc.sync.dma_start(out=out_words, in_=ow[:])
         scale_rows = out_2[0].bitcast(I32)
         for q in range(4):
-            queue = nc.sync if q % 2 == 0 else nc.scalar
+            queue = nc.sync if q == 3 else nc.scalar
             queue.dma_start(out=scale_rows[4 * q : 4 * q + 4, :], in_=osc[32 * q : 32 * q + 4, :].bitcast(I32))

@@ -40,7 +40,7 @@ def tile_picked_fixedpt_tanh_po_kernel(tc, x_words, x_scales, w1_words, w1_scale
     nc = tc.nc
     with ExitStack() as ctx:
         keep = ctx.enter_context(tc.tile_pool(name="keep", bufs=1))
-        ring = ctx.enter_context(tc.tile_pool(name="ring", bufs=3))
+        ring = ctx.enter_context(tc.tile_pool(name="ring", bufs=4))
         psum = ctx.enter_context(tc.psum_pool(name="psum", bufs=1))
 
         offs_t = keep.tile([P, S // 16], U16, name="offs_t")
@@ -51,59 +51,57 @@ def tile_picked_fixedpt_tanh_po_kernel(tc, x_words, x_scales, w1_words, w1_scale
         w1w_raw = keep.tile([P, H], I32, name="w1w_raw", tag="w1w_slot", align_bytes=64)
         w1s_raw = keep.tile([P, H], U8, name="w1s_raw", tag="w1s_slot", align_bytes=64)
         w1w = keep.tile([P, H], I32, name="w1w", align_bytes=64)
-        w1s_first = keep.tile([P, P], U8, name="w1s_first", align_bytes=64)
-        w2w = keep.tile([P, N], I32, name="w2w", align_bytes=64)
+        w1s = keep.tile([P, H], U8, name="w1s", align_bytes=64)
+        w2w_raw = keep.tile([P, N], I32, name="w2w_raw", align_bytes=64)
+        w2s_raw = keep.tile([P, N], U8, name="w2s_raw", align_bytes=64)
+        gain = keep.tile([P, PACK], F32, name="gain", align_bytes=64)
         minus_one = keep.tile([P, V], F32, name="minus_one", align_bytes=64)
         warm = keep.tile([P, 1], F32, name="warm")
         xgs = keep.tile([P, S], U8, name="xgs", align_bytes=64)
-        xgw = keep.tile([P, S], I32, name="xgw", align_bytes=64)
 
-        SPLIT = 288
-        nc.vector.memset(xs[:].bitcast(I32)[:, :SPLIT], 0)
-        nc.gpsimd.memset(xs[:].bitcast(I32)[:, SPLIT:], 0)
+        nc.vector.memset(xs[:].bitcast(I32), 0)
         nc.vector.memset(minus_one[:], -1.0)
-        nc.gpsimd.memset(w1s_raw[:].bitcast(I32), 0)
+        nc.vector.memset(w1s_raw[:].bitcast(I32), 0)
+        nc.vector.memset(w2s_raw[:].bitcast(I32), 0)
 
         nc.sync.dma_start(offs_t[:], offs)
         nc.sync.dma_start(out=w1w_raw[:], in_=as_words(w1_words))
-        nc.sync.dma_start(la_t[:], la)
         load_scale_rows([nc.scalar, nc.scalar, nc.sync, nc.sync], xs, x_scales)
         nc.sync.dma_start(out=xw[:], in_=as_words(x_words))
-        load_scale_rows([nc.sync] * 4, w1s_raw, w1_scales)
-        nc.sync.dma_start(lb_t[:], lb)
         nc.scalar.activation(warm[:], minus_one[:, 0:1], ACT.Tanh)
+        load_scale_rows([nc.sync, nc.sync, nc.scalar, nc.scalar], w1s_raw, w1_scales)
+        nc.sync.dma_start(la_t[:], la)
+        nc.sync.dma_start(out=w2w_raw[:], in_=as_words(w2_words))
+        nc.sync.dma_start(lb_t[:], lb)
+        nc.sync.dma_start(out=gain[:], in_=gn.rearrange("(p t) o -> p (t o)", t=PACK))
+        load_scale_rows([nc.sync] * 4, w2s_raw, w2_scales)
 
         deal(nc, w1w, w1w_raw)
-        w2s_raw = keep.tile([P, N], U8, name="w2s_raw", tag="w1w_slot", align_bytes=64)
-        nc.gpsimd.memset(w2s_raw[:].bitcast(I32), 0)
-        load_scale_rows([nc.scalar] * 4, w2s_raw, w2_scales)
         nc.vector.tensor_copy(xgs[:], xs[:].indirect(offs_t[:]))
-        w2w_raw = keep.tile([P, N], I32, name="w2w_raw", tag="xs_slot", align_bytes=64)
-        nc.sync.dma_start(out=w2w_raw[:], in_=as_words(w2_words))
         HALF = S // 2
-        w1s_by_plane = w1s_raw[:].rearrange("p (m t) -> p m t", t=PACK)
-        nc.vector.tensor_copy(out=w1s_first[:], in_=w1s_by_plane[:, :, 0])
-        for u in range(2):
-            nc.vector.tensor_copy(xgw[:, u * HALF : (u + 1) * HALF].bitcast(U32),
-                                  xw[:].bitcast(U32).indirect(offs_t[:, u * HALF // 16 : (u + 1) * HALF // 16]))
-        w1s_rest = keep.tile([P, (PACK - 1) * P], U8, name="w1s_rest", tag="xw_slot", align_bytes=64)
-        nc.vector.tensor_copy(out=w1s_rest[:].rearrange("p (t m) -> p m t", t=PACK - 1), in_=w1s_by_plane[:, :, 1:])
-        gain = keep.tile([P, PACK], F32, name="gain", tag="w1s_slot", align_bytes=64)
-        nc.sync.dma_start(out=gain[:], in_=gn.rearrange("(p t) o -> p (t o)", t=PACK))
+        halves = [slice(0, HALF), slice(HALF, S)]
+        xgw = [keep.tile([P, HALF], I32, name="xgw0", align_bytes=64)]
+        nc.vector.tensor_copy(xgw[0][:].bitcast(U32), xw[:].bitcast(U32).indirect(offs_t[:, : HALF // 16]))
+        deal(nc, w1s, w1s_raw)
+        xgw.append(keep.tile([P, HALF], I32, name="xgw1", tag="w1s_slot", align_bytes=64))
+        nc.vector.tensor_copy(xgw[1][:].bitcast(U32), xw[:].bitcast(U32).indirect(offs_t[:, HALF // 16 :]))
+        w2w = keep.tile([P, N], I32, name="w2w", tag="xw_slot", align_bytes=64)
         deal(nc, w2w, w2w_raw)
-        w2s = keep.tile([P, N], U8, name="w2s", tag="xs_slot", align_bytes=64)
-        deal(nc, w2s, w2s_raw)
 
         y_ps = {}
         for t in PLANE_ORDER:
             cols = slice(t * P, (t + 1) * P)
-            parts = [slice(0, HALF), slice(HALF, S)] if t == PLANE_ORDER[0] else [slice(0, S)]
-            y_ps[t] = []
-            for u, part in enumerate(parts):
-                bank = psum.tile([P, part.stop - part.start], F32, name="y_ps%d_%d" % (t, u))
-                nc.tensor.matmul_mx(out=bank[:], lhsT=w1w[:, cols].bitcast(FP8X4), lhsT_scale=w1s_first[:] if t == 0 else w1s_rest[:, (t - 1) * P : t * P],
-                                    rhs=xgw[:, part].bitcast(FP8X4), rhs_scale=xgs[:, part], start=True, stop=True)
-                y_ps[t].append((part, bank))
+            if t == PLANE_ORDER[0]:
+                banks = [psum.tile([P, HALF], F32, name="y_ps%d_%d" % (t, u)) for u in range(2)]
+                outs = [bank[:] for bank in banks]
+                y_ps[t] = list(zip(halves, banks))
+            else:
+                bank = psum.tile([P, S], F32, name="y_ps%d_0" % t)
+                outs = [bank[:, half] for half in halves]
+                y_ps[t] = [(slice(0, S), bank)]
+            for u, half in enumerate(halves):
+                nc.tensor.matmul_mx(out=outs[u], lhsT=w1w[:, cols].bitcast(FP8X4), lhsT_scale=w1s[:, cols],
+                                    rhs=xgw[u][:].bitcast(FP8X4), rhs_scale=xgs[:, half], start=True, stop=True)
 
         zb = [keep.tile([P, CHUNK, PACK], BF16, name="zb%d" % c, align_bytes=64) for c in range(CHUNKS)]
         neg_tanh, state, neg_p, y_b = {}, {}, {}, {}
@@ -139,37 +137,30 @@ def tile_picked_fixedpt_tanh_po_kernel(tc, x_words, x_scales, w1_words, w1_scale
             nc.vector.tensor_scalar(zb[c][:, :, t], state[t][:, c * CHUNK : (c + 1) * CHUNK], gain[:, t : t + 1], None, ALU.mult)
 
         a, b, c3, d = PLANE_ORDER
-        for t in (a, b, c3):
+        for t in PLANE_ORDER:
             leave_tanh(t)
             leave_state(t)
-        leave_tanh(d)
         gather_a(a)
         gather_b(a)
         gather_a(b)
         scatter_a(a)
         gather_b(b)
         scatter_b(a)
-        for c in range(CHUNKS):
-            round_scalar(a, c)
-        leave_state(d)
         gather_a(c3)
         scatter_a(b)
         gather_b(c3)
         scatter_b(b)
-        for c in range(CHUNKS):
-            round_scalar(b, c)
         gather_a(d)
         gather_b(d)
         scatter_a(c3)
         scatter_a(d)
         scatter_b(c3)
-        for c in range(CHUNKS):
-            round_scalar(c3, c)
         scatter_b(d)
-        round_vector(d, 0)
-        round_vector(d, 1)
-        round_scalar(d, 2)
-        round_scalar(d, 3)
+        w2s = keep.tile([P, N], U8, name="w2s", tag="y_b%d" % d, align_bytes=64)
+        deal(nc, w2s, w2s_raw)
+        for t in PLANE_ORDER:
+            for c in range(CHUNKS):
+                round_scalar(t, c)
 
         zw = keep.tile([P, S], I32, name="zw", align_bytes=64)
         zs = keep.tile([P, S], U8, name="zs", align_bytes=64)
@@ -192,7 +183,7 @@ def tile_picked_fixedpt_tanh_po_kernel(tc, x_words, x_scales, w1_words, w1_scale
                     m = slice(t * P, (t + 1) * P)
                     nc.tensor.matmul_mx(out=o_ps[:, t - planes.start, :], lhsT=w2w[:, m].bitcast(FP8X4), lhsT_scale=w2s[:, m],
                                         rhs=zw[:, cols].bitcast(FP8X4), rhs_scale=zs[:, cols], start=True, stop=True)
-                if c == 1:
+                if c == 0:
                     nc.vector.tensor_copy(o_sb[:, planes.start : planes.stop, :], o_ps[:])
                 else:
                     nc.scalar.copy(o_sb[:, planes.start : planes.stop, :], o_ps[:])
@@ -211,8 +202,9 @@ def tile_picked_fixedpt_tanh_po_kernel(tc, x_words, x_scales, w1_words, w1_scale
             if c > 0:
                 cols = slice((c - 1) * CHUNK, c * CHUNK)
                 nc.vector.quantize_mx(out=ow[:, cols].bitcast(FP8X4), scales=osc[:, cols], in_=ob[c - 1][:].rearrange("p j t -> p (j t)"))
-        nc.sync.dma_start(out=out_words, in_=ow[:])
+        early, last = slice(0, S - CHUNK), slice(S - CHUNK, S)
+        nc.sync.dma_start(out=out_words[:, early], in_=ow[:, early])
+        nc.sync.dma_start(out=out_words[:, last], in_=ow[:, last])
         scale_rows = out_2[0].bitcast(I32)
-        for q in range(4):
-            queue = nc.sync if q == 3 else nc.scalar
+        for q, queue in enumerate([nc.scalar, nc.scalar, nc.scalar, nc.sync]):
             queue.dma_start(out=scale_rows[4 * q : 4 * q + 4, :], in_=osc[32 * q : 32 * q + 4, :].bitcast(I32))

@@ -36,11 +36,14 @@ def deal(nc, dealt, raw):
     nc.vector.tensor_copy(out=dealt[:].rearrange("p (t m) -> p m t", t=PACK), in_=raw[:].rearrange("p (m t) -> p m t", t=PACK))
 
 
+def deal_bytes(nc, dealt, raw):
+    nc.vector.tensor_copy(out=dealt[:].rearrange("p (t m) -> p t m", t=PACK), in_=raw[:].rearrange("p (m t) -> p t m", t=PACK))
+
+
 def tile_picked_fixedpt_tanh_po_kernel(tc, x_words, x_scales, w1_words, w1_scales, gn, w2_words, w2_scales, offs, la, lb, out_0, out_1, out_2):
     nc = tc.nc
     with ExitStack() as ctx:
         keep = ctx.enter_context(tc.tile_pool(name="keep", bufs=1))
-        ring = ctx.enter_context(tc.tile_pool(name="ring", bufs=4))
         psum = ctx.enter_context(tc.psum_pool(name="psum", bufs=1))
 
         offs_t = keep.tile([P, S // 16], U16, name="offs_t")
@@ -69,7 +72,7 @@ def tile_picked_fixedpt_tanh_po_kernel(tc, x_words, x_scales, w1_words, w1_scale
         load_scale_rows([nc.scalar, nc.scalar, nc.sync, nc.sync], xs, x_scales)
         nc.sync.dma_start(out=xw[:], in_=as_words(x_words))
         nc.scalar.activation(warm[:], minus_one[:, 0:1], ACT.Tanh)
-        load_scale_rows([nc.sync, nc.sync, nc.scalar, nc.scalar], w1s_raw, w1_scales)
+        load_scale_rows([nc.sync] * 4, w1s_raw, w1_scales)
         nc.sync.dma_start(la_t[:], la)
         nc.sync.dma_start(out=w2w_raw[:], in_=as_words(w2_words))
         nc.sync.dma_start(lb_t[:], lb)
@@ -82,7 +85,7 @@ def tile_picked_fixedpt_tanh_po_kernel(tc, x_words, x_scales, w1_words, w1_scale
         halves = [slice(0, HALF), slice(HALF, S)]
         xgw = [keep.tile([P, HALF], I32, name="xgw0", align_bytes=64)]
         nc.vector.tensor_copy(xgw[0][:].bitcast(U32), xw[:].bitcast(U32).indirect(offs_t[:, : HALF // 16]))
-        deal(nc, w1s, w1s_raw)
+        deal_bytes(nc, w1s, w1s_raw)
         xgw.append(keep.tile([P, HALF], I32, name="xgw1", tag="w1s_slot", align_bytes=64))
         nc.vector.tensor_copy(xgw[1][:].bitcast(U32), xw[:].bitcast(U32).indirect(offs_t[:, HALF // 16 :]))
         w2w = keep.tile([P, N], I32, name="w2w", tag="xw_slot", align_bytes=64)
@@ -112,7 +115,7 @@ def tile_picked_fixedpt_tanh_po_kernel(tc, x_words, x_scales, w1_words, w1_scale
                 nc.scalar.activation(neg_tanh[t][:, part], bank[:], ACT.Tanh, scale=-1.0)
 
         def leave_state(t):
-            state[t] = ring.tile([P, S], F32, name="state", align_bytes=64)
+            state[t] = keep.tile([P, S], F32, name="state%d" % t, align_bytes=64)
             for part, bank in y_ps[t]:
                 nc.scalar.copy(state[t][:, part], bank[:])
 
@@ -156,11 +159,16 @@ def tile_picked_fixedpt_tanh_po_kernel(tc, x_words, x_scales, w1_words, w1_scale
         scatter_a(d)
         scatter_b(c3)
         scatter_b(d)
-        w2s = keep.tile([P, N], U8, name="w2s", tag="y_b%d" % d, align_bytes=64)
-        deal(nc, w2s, w2s_raw)
-        for t in PLANE_ORDER:
+        for t in (a, b, c3):
             for c in range(CHUNKS):
                 round_scalar(t, c)
+            if t == a:
+                w2s = keep.tile([P, N], U8, name="w2s", tag="state%d" % a, align_bytes=64)
+                deal_bytes(nc, w2s, w2s_raw)
+        round_vector(d, 0)
+        round_vector(d, 1)
+        round_scalar(d, 2)
+        round_scalar(d, 3)
 
         zw = keep.tile([P, S], I32, name="zw", align_bytes=64)
         zs = keep.tile([P, S], U8, name="zs", align_bytes=64)
@@ -172,23 +180,23 @@ def tile_picked_fixedpt_tanh_po_kernel(tc, x_words, x_scales, w1_words, w1_scale
         for c in range(CHUNKS):
             cols = slice(c * CHUNK, (c + 1) * CHUNK)
             nc.vector.quantize_mx(out=zw[:, cols].bitcast(FP8X4), scales=zs[:, cols], in_=zb[c][:].rearrange("p j t -> p (j t)"))
-        spare = ["y_ps0_0", "y_ps0_1"]
+        bank_names = ["o_ps0", "o_ps1", "o_ps2", "y_ps0_0", "y_ps0_1", "y_ps2_0", "y_ps3_0", "y_ps1_0"]
+        pairs = [range(0, 2), range(2, PACK)]
         for c in range(CHUNKS):
             cols = slice(c * CHUNK, (c + 1) * CHUNK)
-            groups = [range(PACK)] if c < CHUNKS - 1 else [range(0, 2), range(2, PACK)]
             o_sb = keep.tile([P, PACK, CHUNK], F32, name="o_sb%d" % c, align_bytes=64)
-            for g, planes in enumerate(groups):
-                o_ps = psum.tile([P, len(planes), CHUNK], F32, name="o_ps%d" % c if c < CHUNKS - 1 else spare[g])
+            for g, planes in enumerate(pairs):
+                o_ps = psum.tile([P, len(planes), CHUNK], F32, name=bank_names[2 * c + g])
                 for t in planes:
                     m = slice(t * P, (t + 1) * P)
                     nc.tensor.matmul_mx(out=o_ps[:, t - planes.start, :], lhsT=w2w[:, m].bitcast(FP8X4), lhsT_scale=w2s[:, m],
                                         rhs=zw[:, cols].bitcast(FP8X4), rhs_scale=zs[:, cols], start=True, stop=True)
+                nc.scalar.copy(o_sb[:, planes.start : planes.stop, :], o_ps[:])
                 if c == 0:
-                    nc.vector.tensor_copy(o_sb[:, planes.start : planes.stop, :], o_ps[:])
-                else:
-                    nc.scalar.copy(o_sb[:, planes.start : planes.stop, :], o_ps[:])
-            nc.sync.dma_start(out=out_rows[:, :, cols], in_=o_sb[:])
-            res.append((o_sb, groups))
+                    nc.sync.dma_start(out=out_rows[:, planes.start : planes.stop, cols], in_=o_sb[:, planes.start : planes.stop, :])
+            if c > 0:
+                nc.sync.dma_start(out=out_rows[:, :, cols], in_=o_sb[:])
+            res.append((o_sb, pairs if c == CHUNKS - 1 else [range(PACK)]))
         ob = []
         for c in range(CHUNKS + 1):
             if c < CHUNKS:

@@ -107,12 +107,7 @@ def tile_picked_fixedpt_tanh_po_kernel(tc, x_words, x_scales, w1_words, w1_scale
                                     rhs=xgw[u][:].bitcast(FP8X4), rhs_scale=xgs[:, half], start=True, stop=True)
 
         zb = [keep.tile([P, CHUNK, PACK], BF16, name="zb%d" % c, align_bytes=64) for c in range(CHUNKS)]
-        neg_tanh, state, neg_p, y_b = {}, {}, {}, {}
-
-        def leave_tanh(t):
-            neg_tanh[t] = keep.tile([P, S], F32, name="neg_tanh%d" % t, align_bytes=64)
-            for part, bank in y_ps[t]:
-                nc.scalar.activation(neg_tanh[t][:, part], bank[:], ACT.Tanh, scale=-1.0)
+        state, neg_p, y_b = {}, {}, {}
 
         def leave_state(t):
             state[t] = keep.tile([P, S], F32, name="state%d" % t, align_bytes=64)
@@ -120,8 +115,10 @@ def tile_picked_fixedpt_tanh_po_kernel(tc, x_words, x_scales, w1_words, w1_scale
                 nc.scalar.copy(state[t][:, part], bank[:])
 
         def gather_a(t):
+            y_a = keep.tile([P, V], F32, name="y_a%d" % t, align_bytes=64)
+            nc.vector.tensor_copy(y_a[:], state[t][:].indirect(la_t[:]))
             neg_p[t] = keep.tile([P, V], F32, name="neg_p%d" % t, align_bytes=64)
-            nc.vector.tensor_copy(neg_p[t][:], neg_tanh[t][:].indirect(la_t[:]))
+            nc.scalar.activation(neg_p[t][:], y_a[:], ACT.Tanh, scale=-1.0)
 
         def gather_b(t):
             y_b[t] = keep.tile([P, V], F32, name="y_b%d" % t, align_bytes=64)
@@ -141,7 +138,6 @@ def tile_picked_fixedpt_tanh_po_kernel(tc, x_words, x_scales, w1_words, w1_scale
 
         a, b, c3, d = PLANE_ORDER
         for t in PLANE_ORDER:
-            leave_tanh(t)
             leave_state(t)
         gather_a(a)
         gather_b(a)

@@ -114,21 +114,21 @@ def tile_picked_fixedpt_tanh_po_kernel(tc, x_words, x_scales, w1_words, w1_scale
             for part, bank in y_ps[t]:
                 nc.scalar.copy(state[t][:, part], bank[:])
 
-        def gather_a(t):
-            y_a = keep.tile([P, V], F32, name="y_a%d" % t, align_bytes=64)
-            nc.vector.tensor_copy(y_a[:], state[t][:].indirect(la_t[:]))
-            neg_p[t] = keep.tile([P, V], F32, name="neg_p%d" % t, align_bytes=64)
-            nc.scalar.activation(neg_p[t][:], y_a[:], ACT.Tanh, scale=-1.0)
+        def gather_pair(pair):
+            y_a = keep.tile([P, len(pair), V], F32, name="y_a%d" % pair[0], align_bytes=64)
+            neg = keep.tile([P, len(pair), V], F32, name="neg_p%d" % pair[0], align_bytes=64)
+            for i, t in enumerate(pair):
+                nc.vector.tensor_copy(y_a[:, i, :], state[t][:].indirect(la_t[:]))
+                y_b[t] = keep.tile([P, V], F32, name="y_b%d" % t, align_bytes=64)
+                nc.vector.tensor_copy(y_b[t][:], state[t][:].indirect(lb_t[:]))
+                neg_p[t] = neg[:, i, :]
+            nc.scalar.activation(neg[:], y_a[:], ACT.Tanh, scale=-1.0)
 
-        def gather_b(t):
-            y_b[t] = keep.tile([P, V], F32, name="y_b%d" % t, align_bytes=64)
-            nc.vector.tensor_copy(y_b[t][:], state[t][:].indirect(lb_t[:]))
-
-        def scatter_a(t):
-            nc.vector.tensor_tensor(state[t][:].indirect(la_t[:]), neg_p[t][:], minus_one[:], ALU.mult)
-
-        def scatter_b(t):
-            nc.vector.tensor_tensor(state[t][:].indirect(lb_t[:]), y_b[t][:], neg_p[t][:], ALU.add)
+        def scatter_pair(pair):
+            for t in pair:
+                nc.vector.tensor_tensor(state[t][:].indirect(la_t[:]), neg_p[t], minus_one[:], ALU.mult)
+            for t in pair:
+                nc.vector.tensor_tensor(state[t][:].indirect(lb_t[:]), y_b[t][:], neg_p[t], ALU.add)
 
         def round_scalar(t, c):
             nc.scalar.activation(zb[c][:, :, t], state[t][:, c * CHUNK : (c + 1) * CHUNK], ACT.Copy, scale=gain[:, t : t + 1])
@@ -139,22 +139,10 @@ def tile_picked_fixedpt_tanh_po_kernel(tc, x_words, x_scales, w1_words, w1_scale
         a, b, c3, d = PLANE_ORDER
         for t in PLANE_ORDER:
             leave_state(t)
-        gather_a(a)
-        gather_b(a)
-        gather_a(b)
-        scatter_a(a)
-        gather_b(b)
-        scatter_b(a)
-        gather_a(c3)
-        scatter_a(b)
-        gather_b(c3)
-        scatter_b(b)
-        gather_a(d)
-        gather_b(d)
-        scatter_a(c3)
-        scatter_a(d)
-        scatter_b(c3)
-        scatter_b(d)
+        for pair in ((a, b), (c3, d)):
+            gather_pair(pair)
+        for pair in ((a, b), (c3, d)):
+            scatter_pair(pair)
         for t in (a, b, c3):
             for c in range(CHUNKS):
                 round_scalar(t, c)

@@ -107,28 +107,33 @@ def tile_picked_fixedpt_tanh_po_kernel(tc, x_words, x_scales, w1_words, w1_scale
                                     rhs=xgw[u][:].bitcast(FP8X4), rhs_scale=xgs[:, half], start=True, stop=True)
 
         zb = [keep.tile([P, CHUNK, PACK], BF16, name="zb%d" % c, align_bytes=64) for c in range(CHUNKS)]
-        state, neg_p, y_b = {}, {}, {}
+        y_sb, state, neg_p, y_b = {}, {}, {}, {}
 
-        def leave_state(t):
-            state[t] = keep.tile([P, S], F32, name="state%d" % t, align_bytes=64)
+        def leave_psum(t):
+            y_sb[t] = keep.tile([P, S], F32, name="y_sb%d" % t, align_bytes=64)
             for part, bank in y_ps[t]:
-                nc.scalar.copy(state[t][:, part], bank[:])
+                nc.scalar.copy(y_sb[t][:, part], bank[:])
 
-        def gather_pair(pair):
-            y_a = keep.tile([P, len(pair), V], F32, name="y_a%d" % pair[0], align_bytes=64)
-            neg = keep.tile([P, len(pair), V], F32, name="neg_p%d" % pair[0], align_bytes=64)
+        def gather_a(t, slot):
+            y_a = keep.tile([P, V], F32, name="y_a%d" % t, tag=slot, align_bytes=64)
+            nc.vector.tensor_copy(y_a[:], y_sb[t][:].indirect(la_t[:]))
+            neg_p[t] = keep.tile([P, V], F32, name="neg_p%d" % t, align_bytes=64)
+            nc.scalar.activation(neg_p[t][:], y_a[:], ACT.Tanh, scale=-1.0)
+
+        def partners(pair, slot):
+            both = keep.tile([P, len(pair), V], F32, name="y_b%d" % pair[0], tag=slot, align_bytes=64)
             for i, t in enumerate(pair):
-                nc.vector.tensor_copy(y_a[:, i, :], state[t][:].indirect(la_t[:]))
-                y_b[t] = keep.tile([P, V], F32, name="y_b%d" % t, align_bytes=64)
-                nc.vector.tensor_copy(y_b[t][:], state[t][:].indirect(lb_t[:]))
-                neg_p[t] = neg[:, i, :]
-            nc.scalar.activation(neg[:], y_a[:], ACT.Tanh, scale=-1.0)
+                y_b[t] = both[:, i, :]
 
-        def scatter_pair(pair):
-            for t in pair:
-                nc.vector.tensor_tensor(state[t][:].indirect(la_t[:]), neg_p[t], minus_one[:], ALU.mult)
-            for t in pair:
-                nc.vector.tensor_tensor(state[t][:].indirect(lb_t[:]), y_b[t][:], neg_p[t], ALU.add)
+        def gather_b(t):
+            nc.vector.tensor_copy(y_b[t], y_sb[t][:].indirect(lb_t[:]))
+
+        def scatter_a(t):
+            state[t] = keep.tile([P, S], F32, name="state%d" % t, align_bytes=64)
+            nc.vector.tensor_tensor(state[t][:].indirect(la_t[:]), neg_p[t][:], minus_one[:], ALU.mult)
+
+        def scatter_b(t):
+            nc.vector.tensor_tensor(state[t][:].indirect(lb_t[:]), y_b[t], neg_p[t][:], ALU.add)
 
         def round_scalar(t, c):
             nc.scalar.activation(zb[c][:, :, t], state[t][:, c * CHUNK : (c + 1) * CHUNK], ACT.Copy, scale=gain[:, t : t + 1])
@@ -137,18 +142,35 @@ def tile_picked_fixedpt_tanh_po_kernel(tc, x_words, x_scales, w1_words, w1_scale
             nc.vector.tensor_scalar(zb[c][:, :, t], state[t][:, c * CHUNK : (c + 1) * CHUNK], gain[:, t : t + 1], None, ALU.mult)
 
         a, b, c3, d = PLANE_ORDER
-        for t in PLANE_ORDER:
-            leave_state(t)
-        for pair in ((a, b), (c3, d)):
-            gather_pair(pair)
-        for pair in ((a, b), (c3, d)):
-            scatter_pair(pair)
-        for t in (a, b, c3):
+        leave_psum(a)
+        leave_psum(b)
+        gather_a(a, "y_a_first")
+        gather_a(b, "y_a_second")
+        leave_psum(c3)
+        leave_psum(d)
+        partners((a, b), "y_a_second")
+        scatter_a(a)
+        gather_b(a)
+        scatter_a(b)
+        gather_b(b)
+        scatter_b(a)
+        gather_a(c3, "y_sb%d" % a)
+        scatter_b(b)
+        gather_a(d, "y_sb%d" % b)
+        partners((c3, d), "y_sb%d" % b)
+        scatter_a(c3)
+        gather_b(c3)
+        scatter_a(d)
+        gather_b(d)
+        scatter_b(c3)
+        for c in range(CHUNKS):
+            round_scalar(a, c)
+        w2s = keep.tile([P, N], U8, name="w2s", tag="state%d" % a, align_bytes=64)
+        deal_bytes(nc, w2s, w2s_raw)
+        scatter_b(d)
+        for t in (b, c3):
             for c in range(CHUNKS):
                 round_scalar(t, c)
-            if t == a:
-                w2s = keep.tile([P, N], U8, name="w2s", tag="state%d" % a, align_bytes=64)
-                deal_bytes(nc, w2s, w2s_raw)
         round_vector(d, 0)
         round_vector(d, 1)
         round_scalar(d, 2)

@@ -20,6 +20,7 @@ PACK = 4
 CHUNK = 128
 CHUNKS = S // CHUNK
 PLANE_ORDER = (0, 2, 3, 1)
+PIECE = V // 2
 
 
 def as_words(dram):
@@ -58,26 +59,30 @@ def tile_picked_fixedpt_tanh_po_kernel(tc, x_words, x_scales, w1_words, w1_scale
         w2w_raw = keep.tile([P, N], I32, name="w2w_raw", align_bytes=64)
         w2s_raw = keep.tile([P, N], U8, name="w2s_raw", align_bytes=64)
         gain = keep.tile([P, PACK], F32, name="gain", align_bytes=64)
-        minus_one = keep.tile([P, V], F32, name="minus_one", align_bytes=64)
+        warm_in = keep.tile([P, 1], F32, name="warm_in")
         warm = keep.tile([P, 1], F32, name="warm")
+        lanes = keep.tile([P, (2 * PACK - 1) * PIECE], F32, name="lanes", align_bytes=64)
+        last_lane = keep.tile([P, PIECE], F32, name="last_lane", tag="last_lane", align_bytes=64)
         xgs = keep.tile([P, S], U8, name="xgs", align_bytes=64)
 
         nc.vector.memset(xs[:].bitcast(I32), 0)
-        nc.vector.memset(minus_one[:], -1.0)
+        nc.vector.memset(warm_in[:], 0.0)
         nc.vector.memset(w1s_raw[:].bitcast(I32), 0)
         nc.vector.memset(w2s_raw[:].bitcast(I32), 0)
+        nc.vector.memset(lanes[:], -1.0)
+        nc.vector.memset(last_lane[:], -1.0)
 
         nc.sync.dma_start(offs_t[:], offs)
         nc.sync.dma_start(out=w1w_raw[:], in_=as_words(w1_words))
         load_scale_rows([nc.scalar, nc.scalar, nc.sync, nc.sync], xs, x_scales)
         nc.sync.dma_start(out=xw[:], in_=as_words(x_words))
-        nc.scalar.activation(warm[:], minus_one[:, 0:1], ACT.Tanh)
+        nc.scalar.activation(warm[:], warm_in[:], ACT.Tanh)
         load_scale_rows([nc.sync] * 4, w1s_raw, w1_scales)
-        nc.sync.dma_start(la_t[:], la)
         nc.sync.dma_start(out=w2w_raw[:], in_=as_words(w2_words))
+        load_scale_rows([nc.sync] * 4, w2s_raw, w2_scales)
+        nc.sync.dma_start(la_t[:], la)
         nc.sync.dma_start(lb_t[:], lb)
         nc.sync.dma_start(out=gain[:], in_=gn.rearrange("(p t) o -> p (t o)", t=PACK))
-        load_scale_rows([nc.sync] * 4, w2s_raw, w2_scales)
 
         deal(nc, w1w, w1w_raw)
         nc.vector.tensor_copy(xgs[:], xs[:].indirect(offs_t[:]))
@@ -85,8 +90,11 @@ def tile_picked_fixedpt_tanh_po_kernel(tc, x_words, x_scales, w1_words, w1_scale
         halves = [slice(0, HALF), slice(HALF, S)]
         xgw = [keep.tile([P, HALF], I32, name="xgw0", align_bytes=64)]
         nc.vector.tensor_copy(xgw[0][:].bitcast(U32), xw[:].bitcast(U32).indirect(offs_t[:, : HALF // 16]))
-        deal_bytes(nc, w1s, w1s_raw)
-        xgw.append(keep.tile([P, HALF], I32, name="xgw1", tag="w1s_slot", align_bytes=64))
+        dealt_planes = w1s[:].rearrange("p (t m) -> p t m", t=PACK)
+        raw_planes = w1s_raw[:].rearrange("p (m t) -> p t m", t=PACK)
+        for planes in (slice(0, 1), slice(2, 3), slice(1, 4, 2)):
+            nc.gpsimd.tensor_copy(out=dealt_planes[:, planes, :], in_=raw_planes[:, planes, :])
+        xgw.append(keep.tile([P, HALF], I32, name="xgw1", align_bytes=64))
         nc.vector.tensor_copy(xgw[1][:].bitcast(U32), xw[:].bitcast(U32).indirect(offs_t[:, HALF // 16 :]))
         w2w = keep.tile([P, N], I32, name="w2w", tag="xw_slot", align_bytes=64)
         deal(nc, w2w, w2w_raw)
@@ -102,72 +110,98 @@ def tile_picked_fixedpt_tanh_po_kernel(tc, x_words, x_scales, w1_words, w1_scale
                 bank = psum.tile([P, S], F32, name="y_ps%d_0" % t)
                 outs = [bank[:, half] for half in halves]
                 y_ps[t] = [(slice(0, S), bank)]
-            for u, half in enumerate(halves):
+            for u in (0, 1) if t in PLANE_ORDER[:2] else (1, 0):
+                half = halves[u]
                 nc.tensor.matmul_mx(out=outs[u], lhsT=w1w[:, cols].bitcast(FP8X4), lhsT_scale=w1s[:, cols],
                                     rhs=xgw[u][:].bitcast(FP8X4), rhs_scale=xgs[:, half], start=True, stop=True)
 
         zb = [keep.tile([P, CHUNK, PACK], BF16, name="zb%d" % c, align_bytes=64) for c in range(CHUNKS)]
-        y_sb, state, neg_p, y_b = {}, {}, {}, {}
+        y_sb, tanh_sb, state, p_vals, q_vals = {}, {}, {}, {}, {}
 
-        def leave_psum(t):
-            y_sb[t] = keep.tile([P, S], F32, name="y_sb%d" % t, align_bytes=64)
+        def tanh_out_of_psum(t):
+            tanh_sb[t] = keep.tile([P, S], F32, name="tanh_sb%d" % t, align_bytes=64)
+            for part, bank in y_ps[t]:
+                nc.scalar.activation(tanh_sb[t][:, part], bank[:], ACT.Tanh, scale=-1.0)
+
+        def y_out_of_psum(t, slot):
+            y_sb[t] = keep.tile([P, S], F32, name="y_sb%d" % t, tag=slot, align_bytes=64)
             for part, bank in y_ps[t]:
                 nc.scalar.copy(y_sb[t][:, part], bank[:])
 
-        def gather_a(t, slot):
-            y_a = keep.tile([P, V], F32, name="y_a%d" % t, tag=slot, align_bytes=64)
-            nc.vector.tensor_copy(y_a[:], y_sb[t][:].indirect(la_t[:]))
-            neg_p[t] = keep.tile([P, V], F32, name="neg_p%d" % t, align_bytes=64)
-            nc.scalar.activation(neg_p[t][:], y_a[:], ACT.Tanh, scale=-1.0)
+        def entries(lists, part):
+            return lists[:, part.start // 16 : part.stop // 16]
 
-        def partners(pair, slot):
-            both = keep.tile([P, len(pair), V], F32, name="y_b%d" % pair[0], tag=slot, align_bytes=64)
-            for i, t in enumerate(pair):
-                y_b[t] = both[:, i, :]
+        def gather(step, into):
+            t, part, is_b = step
+            if is_b:
+                nc.vector.tensor_copy(into, y_sb[t][:].indirect(entries(lb_t, part)))
+                q_vals[t, part.start] = into
+            else:
+                nc.vector.tensor_copy(into, tanh_sb[t][:].indirect(entries(la_t, part)))
+                p_vals[t, part.start] = into
 
-        def gather_b(t):
-            nc.vector.tensor_copy(y_b[t], y_sb[t][:].indirect(lb_t[:]))
+        def scatter(step, neg_p, other):
+            t, part, is_b = step
+            if t not in state:
+                state[t] = keep.tile([P, S], F32, name="state%d" % t, align_bytes=64)
+            if is_b:
+                nc.vector.tensor_tensor(state[t][:].indirect(entries(lb_t, part)), other, neg_p, ALU.add)
+            else:
+                nc.vector.tensor_tensor(state[t][:].indirect(entries(la_t, part)), neg_p, other, ALU.mult)
 
-        def scatter_a(t):
-            state[t] = keep.tile([P, S], F32, name="state%d" % t, align_bytes=64)
-            nc.vector.tensor_tensor(state[t][:].indirect(la_t[:]), neg_p[t][:], minus_one[:], ALU.mult)
-
-        def scatter_b(t):
-            nc.vector.tensor_tensor(state[t][:].indirect(lb_t[:]), y_b[t], neg_p[t][:], ALU.add)
+        def lane(i, n=1):
+            return last_lane[:] if i == 2 * PACK - 1 else lanes[:, i * PIECE : (i + n) * PIECE]
 
         def round_scalar(t, c):
             nc.scalar.activation(zb[c][:, :, t], state[t][:, c * CHUNK : (c + 1) * CHUNK], ACT.Copy, scale=gain[:, t : t + 1])
 
         def round_vector(t, c):
-            nc.vector.tensor_scalar(zb[c][:, :, t], state[t][:, c * CHUNK : (c + 1) * CHUNK], gain[:, t : t + 1], None, ALU.mult)
+            nc.vector.tensor_scalar(zb[c][:, :, t], state[t][:, c * CHUNK : (c + 1) * CHUNK], gain_last[:], None, ALU.mult)
 
         a, b, c3, d = PLANE_ORDER
-        leave_psum(a)
-        leave_psum(b)
-        gather_a(a, "y_a_first")
-        gather_a(b, "y_a_second")
-        leave_psum(c3)
-        leave_psum(d)
-        partners((a, b), "y_a_second")
-        scatter_a(a)
-        gather_b(a)
-        scatter_a(b)
-        gather_b(b)
-        scatter_b(a)
-        gather_a(c3, "y_sb%d" % a)
-        scatter_b(b)
-        gather_a(d, "y_sb%d" % b)
-        partners((c3, d), "y_sb%d" % b)
-        scatter_a(c3)
-        gather_b(c3)
-        scatter_a(d)
-        gather_b(d)
-        scatter_b(c3)
-        for c in range(CHUNKS):
-            round_scalar(a, c)
-        w2s = keep.tile([P, N], U8, name="w2s", tag="state%d" % a, align_bytes=64)
+        tanh_out_of_psum(a)
+        tanh_out_of_psum(b)
+        y_out_of_psum(a, "y_sb%d" % a)
+        tanh_out_of_psum(c3)
+        y_out_of_psum(b, "y_sb%d" % b)
+        tanh_out_of_psum(d)
+        y_out_of_psum(c3, "y_sb%d" % c3)
+        y_out_of_psum(d, "y_sb%d" % d)
+
+        whole, lo, hi = slice(0, V), slice(0, PIECE), slice(PIECE, V)
+        p_first = keep.tile([P, V], F32, name="p_first", align_bytes=64)
+        p_second = keep.tile([P, PIECE], F32, name="p_second", align_bytes=64)
+        gather((a, whole, False), p_first[:])
+        gather((b, lo, False), p_second[:])
+        p_vals[a, PIECE] = p_first[:, hi]
+        scatter((a, whole, False), p_first[:], lane(0, 2))
+        p_vals[a, 0] = p_first[:, lo]
+        q_first = keep.tile([P, PIECE], F32, name="q_first", tag="tanh_sb%d" % a, align_bytes=64)
+        gather((a, lo, True), q_first[:])
+        freed = lane(0)
+        for i in range(1, PACK):
+            new, old = PLANE_ORDER[i], PLANE_ORDER[i - 1]
+            scatter((new, lo, False), p_vals[new, 0], lane(2 * i))
+            gather((new, hi, False), freed)
+            scatter((old, lo, True), p_vals[old, 0], q_vals[old, 0])
+            gather((old, hi, True), lane(2 * i))
+            scatter((new, hi, False), p_vals[new, PIECE], lane(2 * i + 1))
+            if i + 1 < PACK:
+                gather((PLANE_ORDER[i + 1], lo, False), q_vals[old, 0])
+                scatter((old, hi, True), p_vals[old, PIECE], q_vals[old, PIECE])
+                gather((new, lo, True), lane(2 * i + 1))
+                freed = q_vals[old, PIECE]
+            if i == 1:
+                for c in range(CHUNKS):
+                    round_scalar(a, c)
+                gain_last = keep.tile([P, 1], F32, name="gain_last", tag="state%d" % a, align_bytes=64)
+                nc.scalar.copy(gain_last[:], gain[:, d : d + 1])
+        q_last = keep.tile([P, V], F32, name="q_last", tag="tanh_sb%d" % d, align_bytes=64)
+        gather((d, whole, True), q_last[:])
+        scatter((c3, hi, True), p_vals[c3, PIECE], q_vals[c3, PIECE])
+        w2s = keep.tile([P, N], U8, name="w2s", tag="last_lane", align_bytes=64)
         deal_bytes(nc, w2s, w2s_raw)
-        scatter_b(d)
+        scatter((d, whole, True), lane(3, 2), q_last[:])
         for t in (b, c3):
             for c in range(CHUNKS):
                 round_scalar(t, c)

@@ -20,7 +20,6 @@ PACK = 4
 CHUNK = 128
 CHUNKS = S // CHUNK
 PLANE_ORDER = (0, 2, 3, 1)
-PIECE = V // 2
 
 
 def as_words(dram):
@@ -61,16 +60,14 @@ def tile_picked_fixedpt_tanh_po_kernel(tc, x_words, x_scales, w1_words, w1_scale
         gain = keep.tile([P, PACK], F32, name="gain", align_bytes=64)
         warm_in = keep.tile([P, 1], F32, name="warm_in")
         warm = keep.tile([P, 1], F32, name="warm")
-        lanes = keep.tile([P, (2 * PACK - 1) * PIECE], F32, name="lanes", align_bytes=64)
-        last_lane = keep.tile([P, PIECE], F32, name="last_lane", tag="last_lane", align_bytes=64)
+        minus_one = keep.tile([P, V], F32, name="minus_one", align_bytes=64)
         xgs = keep.tile([P, S], U8, name="xgs", align_bytes=64)
 
         nc.vector.memset(xs[:].bitcast(I32), 0)
         nc.vector.memset(warm_in[:], 0.0)
         nc.vector.memset(w1s_raw[:].bitcast(I32), 0)
         nc.vector.memset(w2s_raw[:].bitcast(I32), 0)
-        nc.vector.memset(lanes[:], -1.0)
-        nc.vector.memset(last_lane[:], -1.0)
+        nc.vector.memset(minus_one[:], -1.0)
 
         nc.sync.dma_start(offs_t[:], offs)
         nc.sync.dma_start(out=w1w_raw[:], in_=as_words(w1_words))
@@ -115,100 +112,84 @@ def tile_picked_fixedpt_tanh_po_kernel(tc, x_words, x_scales, w1_words, w1_scale
                 nc.tensor.matmul_mx(out=outs[u], lhsT=w1w[:, cols].bitcast(FP8X4), lhsT_scale=w1s[:, cols],
                                     rhs=xgw[u][:].bitcast(FP8X4), rhs_scale=xgs[:, half], start=True, stop=True)
 
-        zb = [keep.tile([P, CHUNK, PACK], BF16, name="zb%d" % c, align_bytes=64) for c in range(CHUNKS)]
-        y_sb, tanh_sb, state, p_vals, q_vals = {}, {}, {}, {}, {}
+        def wide(name, slot):
+            return keep.tile([P, S], F32, name=name, tag=slot, align_bytes=64)
 
-        def tanh_out_of_psum(t):
-            tanh_sb[t] = keep.tile([P, S], F32, name="tanh_sb%d" % t, align_bytes=64)
+        def narrow(name, slot):
+            return keep.tile([P, V], F32, name=name, tag=slot, align_bytes=64)
+
+        def out_of_psum(into, t, func, scale):
             for part, bank in y_ps[t]:
-                nc.scalar.activation(tanh_sb[t][:, part], bank[:], ACT.Tanh, scale=-1.0)
+                nc.scalar.activation(into[:, part], bank[:], func, scale=scale)
 
-        def y_out_of_psum(t, slot):
-            y_sb[t] = keep.tile([P, S], F32, name="y_sb%d" % t, tag=slot, align_bytes=64)
-            for part, bank in y_ps[t]:
-                nc.scalar.copy(y_sb[t][:, part], bank[:])
+        def look_up(into, window, lists):
+            nc.scalar.activation(into, window[:].indirect(lists[:]), ACT.Copy)
 
-        def entries(lists, part):
-            return lists[:, part.start // 16 : part.stop // 16]
+        state = {t: keep.tile([P, S], F32, name="state%d" % t, align_bytes=64) for t in PLANE_ORDER}
 
-        def gather(step, into):
-            t, part, is_b = step
-            if is_b:
-                nc.vector.tensor_copy(into, y_sb[t][:].indirect(entries(lb_t, part)))
-                q_vals[t, part.start] = into
-            else:
-                nc.vector.tensor_copy(into, tanh_sb[t][:].indirect(entries(la_t, part)))
-                p_vals[t, part.start] = into
+        def put_p(t, neg_p):
+            nc.vector.tensor_tensor(state[t][:].indirect(la_t[:]), neg_p, minus_one[:], ALU.mult)
 
-        def scatter(step, neg_p, other):
-            t, part, is_b = step
-            if t not in state:
-                state[t] = keep.tile([P, S], F32, name="state%d" % t, align_bytes=64)
-            if is_b:
-                nc.vector.tensor_tensor(state[t][:].indirect(entries(lb_t, part)), other, neg_p, ALU.add)
-            else:
-                nc.vector.tensor_tensor(state[t][:].indirect(entries(la_t, part)), neg_p, other, ALU.mult)
-
-        def lane(i, n=1):
-            return last_lane[:] if i == 2 * PACK - 1 else lanes[:, i * PIECE : (i + n) * PIECE]
-
-        def round_scalar(t, c):
-            nc.scalar.activation(zb[c][:, :, t], state[t][:, c * CHUNK : (c + 1) * CHUNK], ACT.Copy, scale=gain[:, t : t + 1])
-
-        def round_vector(t, c):
-            nc.vector.tensor_scalar(zb[c][:, :, t], state[t][:, c * CHUNK : (c + 1) * CHUNK], gain_last[:], None, ALU.mult)
+        def put_q(t, y_lb, neg_p):
+            nc.vector.tensor_tensor(state[t][:].indirect(lb_t[:]), y_lb, neg_p, ALU.add)
 
         a, b, c3, d = PLANE_ORDER
-        tanh_out_of_psum(a)
-        tanh_out_of_psum(b)
-        y_out_of_psum(a, "y_sb%d" % a)
-        tanh_out_of_psum(c3)
-        y_out_of_psum(b, "y_sb%d" % b)
-        tanh_out_of_psum(d)
-        y_out_of_psum(c3, "y_sb%d" % c3)
-        y_out_of_psum(d, "y_sb%d" % d)
-
-        whole, lo, hi = slice(0, V), slice(0, PIECE), slice(PIECE, V)
-        p_first = keep.tile([P, V], F32, name="p_first", align_bytes=64)
-        p_second = keep.tile([P, PIECE], F32, name="p_second", align_bytes=64)
-        gather((a, whole, False), p_first[:])
-        gather((b, lo, False), p_second[:])
-        p_vals[a, PIECE] = p_first[:, hi]
-        scatter((a, whole, False), p_first[:], lane(0, 2))
-        p_vals[a, 0] = p_first[:, lo]
-        q_first = keep.tile([P, PIECE], F32, name="q_first", tag="tanh_sb%d" % a, align_bytes=64)
-        gather((a, lo, True), q_first[:])
-        freed = lane(0)
-        for i in range(1, PACK):
-            new, old = PLANE_ORDER[i], PLANE_ORDER[i - 1]
-            scatter((new, lo, False), p_vals[new, 0], lane(2 * i))
-            gather((new, hi, False), freed)
-            scatter((old, lo, True), p_vals[old, 0], q_vals[old, 0])
-            gather((old, hi, True), lane(2 * i))
-            scatter((new, hi, False), p_vals[new, PIECE], lane(2 * i + 1))
-            if i + 1 < PACK:
-                gather((PLANE_ORDER[i + 1], lo, False), q_vals[old, 0])
-                scatter((old, hi, True), p_vals[old, PIECE], q_vals[old, PIECE])
-                gather((new, lo, True), lane(2 * i + 1))
-                freed = q_vals[old, PIECE]
-            if i == 1:
-                for c in range(CHUNKS):
-                    round_scalar(a, c)
-                gain_last = keep.tile([P, 1], F32, name="gain_last", tag="state%d" % a, align_bytes=64)
-                nc.scalar.copy(gain_last[:], gain[:, d : d + 1])
-        q_last = keep.tile([P, V], F32, name="q_last", tag="tanh_sb%d" % d, align_bytes=64)
-        gather((d, whole, True), q_last[:])
-        scatter((c3, hi, True), p_vals[c3, PIECE], q_vals[c3, PIECE])
-        w2s = keep.tile([P, N], U8, name="w2s", tag="last_lane", align_bytes=64)
+        neg_p = {t: narrow("neg_p%d" % t, "neg_p%d" % t) for t in PLANE_ORDER}
+        tanh_a = wide("tanh_a", "slot1")
+        out_of_psum(tanh_a, a, ACT.Tanh, -1.0)
+        nc.vector.tensor_copy(neg_p[a][:], tanh_a[:].indirect(la_t[:]))
+        put_p(a, neg_p[a][:])
+        tanh_b = wide("tanh_b", "slot2")
+        out_of_psum(tanh_b, b, ACT.Tanh, -1.0)
+        y_a = wide("y_a", "slot3")
+        out_of_psum(y_a, a, ACT.Copy, 1.0)
+        look_up(neg_p[b][:], tanh_b, la_t)
+        put_p(b, neg_p[b][:])
+        ylb_a = narrow("ylb_a", "ylb_a")
+        look_up(ylb_a[:], y_a, lb_t)
+        put_q(a, ylb_a[:], neg_p[a][:])
+        y_c = wide("y_c", "slot2")
+        out_of_psum(y_c, c3, ACT.Copy, 1.0)
+        y_b = wide("y_b", "slot3")
+        out_of_psum(y_b, b, ACT.Copy, 1.0)
+        yla_c = narrow("yla_c", "slot4")
+        look_up(yla_c[:], y_c, la_t)
+        y_d = wide("y_d", "slot1")
+        out_of_psum(y_d, d, ACT.Copy, 1.0)
+        nc.scalar.activation(neg_p[c3][:], yla_c[:], ACT.Tanh, scale=-1.0)
+        put_p(c3, neg_p[c3][:])
+        ylb_b = narrow("ylb_b", "slot4")
+        look_up(ylb_b[:], y_b, lb_t)
+        put_q(b, ylb_b[:], neg_p[b][:])
+        both = wide("both", "slot5")
+        ylb_c, yla_d = both[:, :V], both[:, V:]
+        look_up(ylb_c, y_c, lb_t)
+        put_q(c3, ylb_c, neg_p[c3][:])
+        look_up(yla_d, y_d, la_t)
+        ylb_d = narrow("ylb_d", "ylb_d")
+        look_up(ylb_d[:], y_d, lb_t)
+        nc.scalar.activation(neg_p[d][:], yla_d, ACT.Tanh, scale=-1.0)
+        put_p(d, neg_p[d][:])
+        w2s = keep.tile([P, N], U8, name="w2s", tag="slot5", align_bytes=64)
         deal_bytes(nc, w2s, w2s_raw)
-        scatter((d, whole, True), lane(3, 2), q_last[:])
-        for t in (b, c3):
-            for c in range(CHUNKS):
-                round_scalar(t, c)
-        round_vector(d, 0)
-        round_vector(d, 1)
-        round_scalar(d, 2)
-        round_scalar(d, 3)
+        put_q(d, ylb_d[:], neg_p[d][:])
+
+        zb = keep.tile([P, S, PACK], BF16, name="zb", tag="slot1", align_bytes=64)
+
+        def round_scalar(t, cols):
+            nc.scalar.activation(zb[:, cols, t], state[t][:, cols], ACT.Copy, scale=gain[:, t : t + 1])
+
+        round_scalar(a, slice(0, S))
+        gain_last = keep.tile([P, 1], F32, name="gain_last", tag="state%d" % a, align_bytes=64)
+        nc.scalar.copy(gain_last[:], gain[:, d : d + 1])
+        round_scalar(b, slice(0, S))
+        round_scalar(c3, slice(0, S))
+        for c in range(CHUNKS):
+            cols = slice(c * CHUNK, (c + 1) * CHUNK)
+            if c < 2:
+                nc.vector.tensor_scalar(zb[:, cols, d], state[d][:, cols], gain_last[:], None, ALU.mult)
+            else:
+                round_scalar(d, cols)
 
         zw = keep.tile([P, S], I32, name="zw", align_bytes=64)
         zs = keep.tile([P, S], U8, name="zs", align_bytes=64)
@@ -219,7 +200,7 @@ def tile_picked_fixedpt_tanh_po_kernel(tc, x_words, x_scales, w1_words, w1_scale
         res = []
         for c in range(CHUNKS):
             cols = slice(c * CHUNK, (c + 1) * CHUNK)
-            nc.vector.quantize_mx(out=zw[:, cols].bitcast(FP8X4), scales=zs[:, cols], in_=zb[c][:].rearrange("p j t -> p (j t)"))
+            nc.vector.quantize_mx(out=zw[:, cols].bitcast(FP8X4), scales=zs[:, cols], in_=zb[:, cols, :].rearrange("p j t -> p (j t)"))
         bank_names = ["o_ps0", "o_ps1", "o_ps2", "y_ps0_0", "y_ps0_1", "y_ps2_0", "y_ps3_0", "y_ps1_0"]
         pairs = [range(0, 2), range(2, PACK)]
         for c in range(CHUNKS):

@@ -36,14 +36,11 @@ def deal(nc, dealt, raw):
     nc.vector.tensor_copy(out=dealt[:].rearrange("p (t m) -> p m t", t=PACK), in_=raw[:].rearrange("p (m t) -> p m t", t=PACK))
 
 
-def deal_bytes(nc, dealt, raw):
-    nc.vector.tensor_copy(out=dealt[:].rearrange("p (t m) -> p t m", t=PACK), in_=raw[:].rearrange("p (m t) -> p t m", t=PACK))
-
-
 def tile_picked_fixedpt_tanh_po_kernel(tc, x_words, x_scales, w1_words, w1_scales, gn, w2_words, w2_scales, offs, la, lb, out_0, out_1, out_2):
     nc = tc.nc
     with ExitStack() as ctx:
         keep = ctx.enter_context(tc.tile_pool(name="keep", bufs=1))
+        row = ctx.enter_context(tc.tile_pool(name="row", bufs=1))
         psum = ctx.enter_context(tc.psum_pool(name="psum", bufs=1))
 
         offs_t = keep.tile([P, S // 16], U16, name="offs_t")
@@ -93,8 +90,6 @@ def tile_picked_fixedpt_tanh_po_kernel(tc, x_words, x_scales, w1_words, w1_scale
             nc.gpsimd.tensor_copy(out=dealt_planes[:, planes, :], in_=raw_planes[:, planes, :])
         xgw.append(keep.tile([P, HALF], I32, name="xgw1", align_bytes=64))
         nc.vector.tensor_copy(xgw[1][:].bitcast(U32), xw[:].bitcast(U32).indirect(offs_t[:, HALF // 16 :]))
-        w2w = keep.tile([P, N], I32, name="w2w", tag="xw_slot", align_bytes=64)
-        deal(nc, w2w, w2w_raw)
 
         y_ps = {}
         for t in PLANE_ORDER:
@@ -112,69 +107,87 @@ def tile_picked_fixedpt_tanh_po_kernel(tc, x_words, x_scales, w1_words, w1_scale
                 nc.tensor.matmul_mx(out=outs[u], lhsT=w1w[:, cols].bitcast(FP8X4), lhsT_scale=w1s[:, cols],
                                     rhs=xgw[u][:].bitcast(FP8X4), rhs_scale=xgs[:, half], start=True, stop=True)
 
-        def wide(name, slot):
-            return keep.tile([P, S], F32, name=name, tag=slot, align_bytes=64)
+        def placed(name, width, dtype, offset):
+            return row.tile([P, width], dtype, name=name, offset=offset, align_bytes=64)
 
-        def narrow(name, slot):
-            return keep.tile([P, V], F32, name=name, tag=slot, align_bytes=64)
+        def narrow(name):
+            return keep.tile([P, V], F32, name=name, align_bytes=64)
 
         def out_of_psum(into, t, func, scale):
             for part, bank in y_ps[t]:
                 nc.scalar.activation(into[:, part], bank[:], func, scale=scale)
 
         def look_up(into, window, lists):
-            nc.scalar.activation(into, window[:].indirect(lists[:]), ACT.Copy)
+            nc.scalar.activation(into[:], window[:].indirect(lists[:]), ACT.Copy)
 
         state = {t: keep.tile([P, S], F32, name="state%d" % t, align_bytes=64) for t in PLANE_ORDER}
+        neg_p = {t: narrow("neg_p%d" % t) for t in PLANE_ORDER[:-1]}
 
-        def put_p(t, neg_p):
-            nc.vector.tensor_tensor(state[t][:].indirect(la_t[:]), neg_p, minus_one[:], ALU.mult)
+        def put_p(t):
+            nc.vector.tensor_tensor(state[t][:].indirect(la_t[:]), neg_p[t][:], minus_one[:], ALU.mult)
 
-        def put_q(t, y_lb, neg_p):
-            nc.vector.tensor_tensor(state[t][:].indirect(lb_t[:]), y_lb, neg_p, ALU.add)
+        def put_q(t, y_lb):
+            nc.vector.tensor_tensor(state[t][:].indirect(lb_t[:]), y_lb[:], neg_p[t][:], ALU.add)
+
+        w2w, w2s = {}, {}
+
+        def deal_words(t, offset):
+            w2w[t] = placed("w2w%d" % t, P, I32, offset)
+            nc.vector.tensor_copy(out=w2w[t][:], in_=w2w_raw[:, t::PACK])
+
+        def deal_scales(t, offset):
+            w2s[t] = placed("w2s%d" % t, P, U8, offset)
+            nc.vector.tensor_copy(out=w2s[t][:], in_=w2s_raw[:, t::PACK])
 
         a, b, c3, d = PLANE_ORDER
-        neg_p = {t: narrow("neg_p%d" % t, "neg_p%d" % t) for t in PLANE_ORDER}
-        tanh_a = wide("tanh_a", "slot1")
+        R1, R2, R3, R4, R5, R6 = 0, 6656, 3840, 9216, 10752, 15360
+        deal_words(0, R6)
+        tanh_a = placed("tanh_a", S, F32, R1)
         out_of_psum(tanh_a, a, ACT.Tanh, -1.0)
         nc.vector.tensor_copy(neg_p[a][:], tanh_a[:].indirect(la_t[:]))
-        put_p(a, neg_p[a][:])
-        tanh_b = wide("tanh_b", "slot2")
+        put_p(a)
+        deal_words(1, R1)
+        tanh_b = placed("tanh_b", S, F32, R2)
         out_of_psum(tanh_b, b, ACT.Tanh, -1.0)
-        y_a = wide("y_a", "slot3")
+        y_a = placed("y_a", S, F32, R3)
         out_of_psum(y_a, a, ACT.Copy, 1.0)
-        look_up(neg_p[b][:], tanh_b, la_t)
-        put_p(b, neg_p[b][:])
-        ylb_a = narrow("ylb_a", "ylb_a")
-        look_up(ylb_a[:], y_a, lb_t)
-        put_q(a, ylb_a[:], neg_p[a][:])
-        y_c = wide("y_c", "slot2")
+        look_up(neg_p[b], tanh_b, la_t)
+        put_p(b)
+        deal_words(2, R2)
+        ylb_a = narrow("ylb_a")
+        look_up(ylb_a, y_a, lb_t)
+        put_q(a, ylb_a)
+        deal_words(3, R3 + 256)
+        y_c = placed("y_c", S, F32, R2 + 512)
         out_of_psum(y_c, c3, ACT.Copy, 1.0)
-        y_b = wide("y_b", "slot3")
+        y_b = placed("y_b", S, F32, R3 + 768)
         out_of_psum(y_b, b, ACT.Copy, 1.0)
-        yla_c = narrow("yla_c", "slot4")
-        look_up(yla_c[:], y_c, la_t)
-        y_d = wide("y_d", "slot1")
+        yla_c = placed("yla_c", V, F32, R4)
+        look_up(yla_c, y_c, la_t)
+        y_d = placed("y_d", S, F32, R3 + 256 - 2048)
         out_of_psum(y_d, d, ACT.Copy, 1.0)
         nc.scalar.activation(neg_p[c3][:], yla_c[:], ACT.Tanh, scale=-1.0)
-        put_p(c3, neg_p[c3][:])
-        ylb_b = narrow("ylb_b", "slot4")
-        look_up(ylb_b[:], y_b, lb_t)
-        put_q(b, ylb_b[:], neg_p[b][:])
-        both = wide("both", "slot5")
-        ylb_c, yla_d = both[:, :V], both[:, V:]
+        put_p(c3)
+        deal_scales(0, R4)
+        ylb_b = placed("ylb_b", V, F32, R4 + 512)
+        look_up(ylb_b, y_b, lb_t)
+        put_q(b, ylb_b)
+        deal_scales(1, R3 + 2304)
+        ylb_c = placed("ylb_c", V, F32, R3 + 768)
         look_up(ylb_c, y_c, lb_t)
-        put_q(c3, ylb_c, neg_p[c3][:])
+        put_q(c3, ylb_c)
+        deal_scales(2, R2 + 2048)
+        yla_d = placed("yla_d", V, F32, R5 + 3584)
         look_up(yla_d, y_d, la_t)
-        ylb_d = narrow("ylb_d", "ylb_d")
-        look_up(ylb_d[:], y_d, lb_t)
-        nc.scalar.activation(neg_p[d][:], yla_d, ACT.Tanh, scale=-1.0)
-        put_p(d, neg_p[d][:])
-        w2s = keep.tile([P, N], U8, name="w2s", tag="slot5", align_bytes=64)
-        deal_bytes(nc, w2s, w2s_raw)
-        put_q(d, ylb_d[:], neg_p[d][:])
+        ylb_d = narrow("ylb_d")
+        look_up(ylb_d, y_d, lb_t)
+        neg_p[d] = placed("neg_p_last", V, F32, R2 + 512)
+        nc.scalar.activation(neg_p[d][:], yla_d[:], ACT.Tanh, scale=-1.0)
+        put_p(d)
+        deal_scales(3, R5 + 4096)
+        put_q(d, ylb_d)
 
-        zb = keep.tile([P, S, PACK], BF16, name="zb", tag="slot1", align_bytes=64)
+        zb = row.tile([P, S, PACK], BF16, name="zb", offset=R5, align_bytes=64)
 
         def round_scalar(t, cols):
             nc.scalar.activation(zb[:, cols, t], state[t][:, cols], ACT.Copy, scale=gain[:, t : t + 1])
@@ -209,8 +222,7 @@ def tile_picked_fixedpt_tanh_po_kernel(tc, x_words, x_scales, w1_words, w1_scale
             for g, planes in enumerate(pairs):
                 o_ps = psum.tile([P, len(planes), CHUNK], F32, name=bank_names[2 * c + g])
                 for t in planes:
-                    m = slice(t * P, (t + 1) * P)
-                    nc.tensor.matmul_mx(out=o_ps[:, t - planes.start, :], lhsT=w2w[:, m].bitcast(FP8X4), lhsT_scale=w2s[:, m],
+                    nc.tensor.matmul_mx(out=o_ps[:, t - planes.start, :], lhsT=w2w[t][:].bitcast(FP8X4), lhsT_scale=w2s[t][:],
                                         rhs=zw[:, cols].bitcast(FP8X4), rhs_scale=zs[:, cols], start=True, stop=True)
                 nc.scalar.copy(o_sb[:, planes.start : planes.stop, :], o_ps[:])
                 if c == 0:

@@ -89,23 +89,30 @@ def tile_picked_fixedpt_tanh_po_kernel(tc, x_words, x_scales, w1_words, w1_scale
         for planes in (slice(0, 1), slice(2, 3), slice(1, 4, 2)):
             nc.gpsimd.tensor_copy(out=dealt_planes[:, planes, :], in_=raw_planes[:, planes, :])
         xgw.append(keep.tile([P, HALF], I32, name="xgw1", align_bytes=64))
-        nc.vector.tensor_copy(xgw[1][:].bitcast(U32), xw[:].bitcast(U32).indirect(offs_t[:, HALF // 16 :]))
+        for first in (0, CHUNK):
+            nc.vector.tensor_copy(xgw[1][:, first : first + CHUNK].bitcast(U32),
+                                  xw[:].bitcast(U32).indirect(offs_t[:, (HALF + first) // 16 : (HALF + first + CHUNK) // 16]))
+
+        def first_product(out, t, part):
+            u = part.start // HALF
+            cols = slice(t * P, (t + 1) * P)
+            nc.tensor.matmul_mx(out=out, lhsT=w1w[:, cols].bitcast(FP8X4), lhsT_scale=w1s[:, cols],
+                                rhs=xgw[u][:, part.start - u * HALF : part.stop - u * HALF].bitcast(FP8X4), rhs_scale=xgs[:, part],
+                                start=True, stop=True)
 
         y_ps = {}
         for t in PLANE_ORDER:
-            cols = slice(t * P, (t + 1) * P)
             if t == PLANE_ORDER[0]:
-                banks = [psum.tile([P, HALF], F32, name="y_ps%d_%d" % (t, u)) for u in range(2)]
-                outs = [bank[:] for bank in banks]
-                y_ps[t] = list(zip(halves, banks))
+                y_ps[t] = []
+                for n, part in enumerate([halves[0], slice(HALF, HALF + CHUNK), slice(HALF + CHUNK, S)]):
+                    bank = psum.tile([P, part.stop - part.start], F32, name="y_ps%d_%d" % (t, n))
+                    first_product(bank[:], t, part)
+                    y_ps[t].append((part, bank))
             else:
                 bank = psum.tile([P, S], F32, name="y_ps%d_0" % t)
-                outs = [bank[:, half] for half in halves]
                 y_ps[t] = [(slice(0, S), bank)]
-            for u in (0, 1) if t in PLANE_ORDER[:2] else (1, 0):
-                half = halves[u]
-                nc.tensor.matmul_mx(out=outs[u], lhsT=w1w[:, cols].bitcast(FP8X4), lhsT_scale=w1s[:, cols],
-                                    rhs=xgw[u][:].bitcast(FP8X4), rhs_scale=xgs[:, half], start=True, stop=True)
+                for half in halves if t == PLANE_ORDER[1] else halves[::-1]:
+                    first_product(bank[:, half], t, half)
 
         def placed(name, width, dtype, offset):
             return row.tile([P, width], dtype, name=name, offset=offset, align_bytes=64)
@@ -140,7 +147,7 @@ def tile_picked_fixedpt_tanh_po_kernel(tc, x_words, x_scales, w1_words, w1_scale
             nc.vector.tensor_copy(out=w2s[t][:], in_=w2s_raw[:, t::PACK])
 
         a, b, c3, d = PLANE_ORDER
-        R1, R2, R3, R4, R5, R6 = 0, 6656, 3840, 9216, 10752, 15360
+        R1, R2, R3, R4, R5, R6 = 0, 4864, 2048, 9216, 10752, 15360
         deal_words(0, R6)
         tanh_a = placed("tanh_a", S, F32, R1)
         out_of_psum(tanh_a, a, ACT.Tanh, -1.0)
@@ -164,15 +171,15 @@ def tile_picked_fixedpt_tanh_po_kernel(tc, x_words, x_scales, w1_words, w1_scale
         out_of_psum(y_b, b, ACT.Copy, 1.0)
         yla_c = placed("yla_c", V, F32, R4)
         look_up(yla_c, y_c, la_t)
-        y_d = placed("y_d", S, F32, R3 + 256 - 2048)
-        out_of_psum(y_d, d, ACT.Copy, 1.0)
         nc.scalar.activation(neg_p[c3][:], yla_c[:], ACT.Tanh, scale=-1.0)
         put_p(c3)
-        deal_scales(0, R4)
+        deal_scales(0, R4 + 256)
         ylb_b = placed("ylb_b", V, F32, R4 + 512)
         look_up(ylb_b, y_b, lb_t)
         put_q(b, ylb_b)
         deal_scales(1, R3 + 2304)
+        y_d = placed("y_d", S, F32, R4 + 256 - 2048)
+        out_of_psum(y_d, d, ACT.Copy, 1.0)
         ylb_c = placed("ylb_c", V, F32, R3 + 768)
         look_up(ylb_c, y_c, lb_t)
         put_q(c3, ylb_c)
@@ -214,7 +221,7 @@ def tile_picked_fixedpt_tanh_po_kernel(tc, x_words, x_scales, w1_words, w1_scale
         for c in range(CHUNKS):
             cols = slice(c * CHUNK, (c + 1) * CHUNK)
             nc.vector.quantize_mx(out=zw[:, cols].bitcast(FP8X4), scales=zs[:, cols], in_=zb[:, cols, :].rearrange("p j t -> p (j t)"))
-        bank_names = ["o_ps0", "o_ps1", "o_ps2", "y_ps0_0", "y_ps0_1", "y_ps2_0", "y_ps3_0", "y_ps1_0"]
+        bank_names = ["o_ps0", "o_ps1", "y_ps0_0", "y_ps0_1", "y_ps0_2", "y_ps2_0", "y_ps3_0", "y_ps1_0"]
         pairs = [range(0, 2), range(2, PACK)]
         for c in range(CHUNKS):
             cols = slice(c * CHUNK, (c + 1) * CHUNK)

@@ -26,9 +26,9 @@ def as_words(dram):
     return dram[0].rearrange("p n t -> p (n t)").bitcast(I32)
 
 
-def load_scale_rows(queues, tile, dram):
+def load_scale_rows(queues, tile, dram, first=0):
     rows = dram[0].bitcast(I32)
-    for q, queue in enumerate(queues):
+    for q, queue in enumerate(queues, first):
         queue.dma_start(out=tile[32 * q : 32 * q + 4, :].bitcast(I32), in_=rows[4 * q : 4 * q + 4, :])
 
 
@@ -60,18 +60,19 @@ def tile_picked_fixedpt_tanh_po_kernel(tc, x_words, x_scales, w1_words, w1_scale
         minus_one = keep.tile([P, V], F32, name="minus_one", align_bytes=64)
         xgs = keep.tile([P, S], U8, name="xgs", align_bytes=64)
 
+        nc.gpsimd.memset(w1s_raw[:].bitcast(I32), 0)
         nc.vector.memset(xs[:].bitcast(I32), 0)
         nc.vector.memset(warm_in[:], 0.0)
-        nc.vector.memset(w1s_raw[:].bitcast(I32), 0)
         nc.vector.memset(w2s_raw[:].bitcast(I32), 0)
         nc.vector.memset(minus_one[:], -1.0)
 
         nc.sync.dma_start(offs_t[:], offs)
+        load_scale_rows([nc.scalar], w1s_raw, w1_scales)
         nc.sync.dma_start(out=w1w_raw[:], in_=as_words(w1_words))
         load_scale_rows([nc.scalar, nc.scalar, nc.sync, nc.sync], xs, x_scales)
         nc.sync.dma_start(out=xw[:], in_=as_words(x_words))
         nc.scalar.activation(warm[:], warm_in[:], ACT.Tanh)
-        load_scale_rows([nc.sync] * 4, w1s_raw, w1_scales)
+        load_scale_rows([nc.sync] * 3, w1s_raw, w1_scales, first=1)
         nc.sync.dma_start(out=w2w_raw[:], in_=as_words(w2_words))
         load_scale_rows([nc.sync] * 4, w2s_raw, w2_scales)
         nc.sync.dma_start(la_t[:], la)

@@ -74,9 +74,10 @@ def tile_picked_fixedpt_tanh_po_kernel(tc, x_words, x_scales, w1_words, w1_scale
         nc.scalar.activation(warm[:], warm_in[:], ACT.Tanh)
         load_scale_rows([nc.sync] * 3, w1s_raw, w1_scales, first=1)
         nc.sync.dma_start(out=w2w_raw[:], in_=as_words(w2_words))
-        load_scale_rows([nc.sync] * 4, w2s_raw, w2_scales)
+        load_scale_rows([nc.sync] * 2, w2s_raw, w2_scales)
         nc.sync.dma_start(la_t[:], la)
         nc.sync.dma_start(lb_t[:], lb)
+        load_scale_rows([nc.sync] * 2, w2s_raw, w2_scales, first=2)
         nc.sync.dma_start(out=gain[:], in_=gn.rearrange("(p t) o -> p (t o)", t=PACK))
 
         deal(nc, w1w, w1w_raw)
@@ -227,8 +228,9 @@ def tile_picked_fixedpt_tanh_po_kernel(tc, x_words, x_scales, w1_words, w1_scale
         for c in range(CHUNKS):
             cols = slice(c * CHUNK, (c + 1) * CHUNK)
             o_sb = keep.tile([P, PACK, CHUNK], F32, name="o_sb%d" % c, align_bytes=64)
-            for g, planes in enumerate(pairs):
-                o_ps = psum.tile([P, len(planes), CHUNK], F32, name=bank_names[2 * c + g])
+            groups = pairs if c < CHUNKS - 1 else [pairs[0], range(2, 3), range(3, PACK)]
+            for g, planes in enumerate(groups):
+                o_ps = psum.tile([P, len(planes), CHUNK], F32, name=bank_names[(2 * c + g) % len(bank_names)])
                 for t in planes:
                     nc.tensor.matmul_mx(out=o_ps[:, t - planes.start, :], lhsT=w2w[t][:].bitcast(FP8X4), lhsT_scale=w2s[t][:],
                                         rhs=zw[:, cols].bitcast(FP8X4), rhs_scale=zs[:, cols], start=True, stop=True)
@@ -238,20 +240,25 @@ def tile_picked_fixedpt_tanh_po_kernel(tc, x_words, x_scales, w1_words, w1_scale
             if c > 0:
                 nc.sync.dma_start(out=out_rows[:, :, cols], in_=o_sb[:])
             res.append((o_sb, pairs if c == CHUNKS - 1 else [range(PACK)]))
-        ob = []
-        for c in range(CHUNKS + 1):
-            if c < CHUNKS:
-                o_bf = keep.tile([P, CHUNK, PACK], BF16, name="o_bf%d" % c, align_bytes=64)
-                o_sb, groups = res[c]
-                for planes in groups:
-                    part = slice(planes.start, planes.stop)
-                    nc.vector.tensor_copy(out=o_bf[:, :, part].rearrange("p (g i) t -> p g t i", i=4),
-                                          in_=o_sb[:, part, :].rearrange("p t (g i) -> p g t i", i=4))
-                ob.append(o_bf)
-            if c > 0:
-                cols = slice((c - 1) * CHUNK, c * CHUNK)
-                nc.vector.quantize_mx(out=ow[:, cols].bitcast(FP8X4), scales=osc[:, cols], in_=ob[c - 1][:].rearrange("p j t -> p (j t)"))
-        early, last = slice(0, S - CHUNK), slice(S - CHUNK, S)
+        o_bf = [keep.tile([P, CHUNK, PACK], BF16, name="o_bf%d" % c, align_bytes=64) for c in range(CHUNKS)]
+
+        def weave(c):
+            o_sb, groups = res[c]
+            for planes in groups:
+                part = slice(planes.start, planes.stop)
+                nc.vector.tensor_copy(out=o_bf[c][:, :, part].rearrange("p (g i) t -> p g t i", i=4),
+                                      in_=o_sb[:, part, :].rearrange("p t (g i) -> p g t i", i=4))
+
+        def quantise_out(c):
+            cols = slice(c * CHUNK, (c + 1) * CHUNK)
+            nc.vector.quantize_mx(out=ow[:, cols].bitcast(FP8X4), scales=osc[:, cols], in_=o_bf[c][:].rearrange("p j t -> p (j t)"))
+
+        for first in range(0, CHUNKS, 2):
+            weave(first)
+            weave(first + 1)
+            quantise_out(first)
+            quantise_out(first + 1)
+        early, last = halves
         nc.sync.dma_start(out=out_words[:, early], in_=ow[:, early])
         nc.sync.dma_start(out=out_words[:, last], in_=ow[:, last])
         scale_rows = out_2[0].bitcast(I32)

@@ -149,7 +149,7 @@ def tile_picked_fixedpt_tanh_po_kernel(tc, x_words, x_scales, w1_words, w1_scale
             nc.vector.tensor_copy(out=w2s[t][:], in_=w2s_raw[:, t::PACK])
 
         a, b, c3, d = PLANE_ORDER
-        R1, R2, R3, R4, R5, R6 = 0, 4864, 2048, 9216, 10752, 15360
+        R1, R3, R4, R5, R2, R6 = 0, 2048, 6400, 7936, 9472, 15616
         deal_words(0, R6)
         tanh_a = placed("tanh_a", S, F32, R1)
         out_of_psum(tanh_a, a, ACT.Tanh, -1.0)
@@ -166,10 +166,10 @@ def tile_picked_fixedpt_tanh_po_kernel(tc, x_words, x_scales, w1_words, w1_scale
         ylb_a = narrow("ylb_a")
         look_up(ylb_a, y_a, lb_t)
         put_q(a, ylb_a)
-        deal_words(3, R3 + 256)
+        deal_words(3, R3)
         y_c = placed("y_c", S, F32, R2 + 512)
         out_of_psum(y_c, c3, ACT.Copy, 1.0)
-        y_b = placed("y_b", S, F32, R3 + 768)
+        y_b = placed("y_b", S, F32, R3 + 512)
         out_of_psum(y_b, b, ACT.Copy, 1.0)
         yla_c = placed("yla_c", V, F32, R4)
         look_up(yla_c, y_c, la_t)
@@ -179,24 +179,24 @@ def tile_picked_fixedpt_tanh_po_kernel(tc, x_words, x_scales, w1_words, w1_scale
         ylb_b = placed("ylb_b", V, F32, R4 + 512)
         look_up(ylb_b, y_b, lb_t)
         put_q(b, ylb_b)
-        deal_scales(1, R3 + 2304)
+        deal_scales(1, R3 + 1536)
         y_d = placed("y_d", S, F32, R4 + 256 - 2048)
         out_of_psum(y_d, d, ACT.Copy, 1.0)
-        ylb_c = placed("ylb_c", V, F32, R3 + 768)
-        look_up(ylb_c, y_c, lb_t)
-        put_q(c3, ylb_c)
-        deal_scales(2, R2 + 2048)
-        yla_d = placed("yla_d", V, F32, R5 + 3584)
+        yla_d = placed("yla_d", V, F32, R5)
         look_up(yla_d, y_d, la_t)
-        ylb_d = narrow("ylb_d")
-        look_up(ylb_d, y_d, lb_t)
-        neg_p[d] = placed("neg_p_last", V, F32, R2 + 512)
+        neg_p[d] = placed("neg_p_last", V, F32, R3 + 512)
         nc.scalar.activation(neg_p[d][:], yla_d[:], ACT.Tanh, scale=-1.0)
         put_p(d)
-        deal_scales(3, R5 + 4096)
+        deal_scales(2, R5)
+        ylb_c = placed("ylb_c", V, F32, R5 + 512)
+        look_up(ylb_c, y_c, lb_t)
+        put_q(c3, ylb_c)
+        deal_scales(3, R2 + 1536)
+        ylb_d = placed("ylb_d", V, F32, R2 + 512)
+        look_up(ylb_d, y_d, lb_t)
         put_q(d, ylb_d)
 
-        zb = row.tile([P, S, PACK], BF16, name="zb", offset=R5, align_bytes=64)
+        zb = row.tile([P, S, PACK], BF16, name="zb", offset=R2 + 2048, align_bytes=64)
 
         def round_scalar(t, cols):
             nc.scalar.activation(zb[:, cols, t], state[t][:, cols], ACT.Copy, scale=gain[:, t : t + 1])
@@ -205,7 +205,8 @@ def tile_picked_fixedpt_tanh_po_kernel(tc, x_words, x_scales, w1_words, w1_scale
         gain_last = keep.tile([P, 1], F32, name="gain_last", tag="state%d" % a, align_bytes=64)
         nc.scalar.copy(gain_last[:], gain[:, d : d + 1])
         round_scalar(b, slice(0, S))
-        round_scalar(c3, slice(0, S))
+        for half in halves:
+            round_scalar(c3, half)
         for c in range(CHUNKS):
             cols = slice(c * CHUNK, (c + 1) * CHUNK)
             if c < 2:

@@ -74,8 +74,8 @@ def tile_picked_fixedpt_tanh_po_kernel(tc, x_words, x_scales, w1_words, w1_scale
         nc.scalar.activation(warm[:], warm_in[:], ACT.Tanh)
         load_scale_rows([nc.sync] * 3, w1s_raw, w1_scales, first=1)
         nc.sync.dma_start(out=w2w_raw[:], in_=as_words(w2_words))
-        load_scale_rows([nc.sync] * 2, w2s_raw, w2_scales)
         nc.sync.dma_start(la_t[:], la)
+        load_scale_rows([nc.sync] * 2, w2s_raw, w2_scales)
         nc.sync.dma_start(lb_t[:], lb)
         load_scale_rows([nc.sync] * 2, w2s_raw, w2_scales, first=2)
         nc.sync.dma_start(out=gain[:], in_=gn.rearrange("(p t) o -> p (t o)", t=PACK))
@@ -113,7 +113,7 @@ def tile_picked_fixedpt_tanh_po_kernel(tc, x_words, x_scales, w1_words, w1_scale
             else:
                 bank = psum.tile([P, S], F32, name="y_ps%d_0" % t)
                 y_ps[t] = [(slice(0, S), bank)]
-                for half in halves if t == PLANE_ORDER[1] else halves[::-1]:
+                for half in halves[::-1]:
                     first_product(bank[:, half], t, half)
 
         def placed(name, width, dtype, offset):
@@ -149,11 +149,12 @@ def tile_picked_fixedpt_tanh_po_kernel(tc, x_words, x_scales, w1_words, w1_scale
             nc.vector.tensor_copy(out=w2s[t][:], in_=w2s_raw[:, t::PACK])
 
         a, b, c3, d = PLANE_ORDER
-        R1, R3, R4, R5, R2, R6 = 0, 2048, 6400, 7936, 9472, 15616
+        R3, R4, R5, R1, R2, R6 = 0, 4352, 5888, 7424, 9408, 15552
         deal_words(0, R6)
         tanh_a = placed("tanh_a", S, F32, R1)
         out_of_psum(tanh_a, a, ACT.Tanh, -1.0)
-        nc.vector.tensor_copy(neg_p[a][:], tanh_a[:].indirect(la_t[:]))
+        nc.vector.tensor_copy(neg_p[a][:, : V // 2], tanh_a[:].indirect(la_t[:, : V // 32]))
+        nc.scalar.activation(neg_p[a][:, V // 2 :], tanh_a[:].indirect(la_t[:, V // 32 :]), ACT.Copy)
         put_p(a)
         deal_words(1, R1)
         tanh_b = placed("tanh_b", S, F32, R2)

@@ -26,9 +26,9 @@ def as_words(dram):
     return dram[0].rearrange("p n t -> p (n t)").bitcast(I32)
 
 
-def load_scale_rows(queues, tile, dram, first=0):
+def load_scale_rows(queue, tile, dram, quadrants):
     rows = dram[0].bitcast(I32)
-    for q, queue in enumerate(queues, first):
+    for q in quadrants:
         queue.dma_start(out=tile[32 * q : 32 * q + 4, :].bitcast(I32), in_=rows[4 * q : 4 * q + 4, :])
 
 
@@ -67,17 +67,17 @@ def tile_picked_fixedpt_tanh_po_kernel(tc, x_words, x_scales, w1_words, w1_scale
         nc.vector.memset(minus_one[:], -1.0)
 
         nc.sync.dma_start(offs_t[:], offs)
-        load_scale_rows([nc.scalar], w1s_raw, w1_scales)
+        load_scale_rows(nc.scalar, w1s_raw, w1_scales, [0])
         nc.sync.dma_start(out=w1w_raw[:], in_=as_words(w1_words))
-        load_scale_rows([nc.scalar, nc.scalar, nc.sync, nc.sync], xs, x_scales)
+        load_scale_rows(nc.sync, xs, x_scales, [0, 2, 1, 3])
         nc.sync.dma_start(out=xw[:], in_=as_words(x_words))
         nc.scalar.activation(warm[:], warm_in[:], ACT.Tanh)
-        load_scale_rows([nc.sync] * 3, w1s_raw, w1_scales, first=1)
+        load_scale_rows(nc.sync, w1s_raw, w1_scales, [1, 2, 3])
         nc.sync.dma_start(out=w2w_raw[:], in_=as_words(w2_words))
         nc.sync.dma_start(la_t[:], la)
-        load_scale_rows([nc.sync] * 2, w2s_raw, w2_scales)
+        load_scale_rows(nc.sync, w2s_raw, w2_scales, [0, 1])
         nc.sync.dma_start(lb_t[:], lb)
-        load_scale_rows([nc.sync] * 2, w2s_raw, w2_scales, first=2)
+        load_scale_rows(nc.sync, w2s_raw, w2_scales, [2, 3])
         nc.sync.dma_start(out=gain[:], in_=gn.rearrange("(p t) o -> p (t o)", t=PACK))
 
         deal(nc, w1w, w1w_raw)

@@ -67,14 +67,17 @@ def tile_picked_fixedpt_tanh_po_kernel(tc, x_words, x_scales, w1_words, w1_scale
         nc.vector.memset(minus_one[:], -1.0)
 
         nc.sync.dma_start(offs_t[:], offs)
-        load_scale_rows(nc.scalar, w1s_raw, w1_scales, [0])
+        nc.scalar.dma_start(out=w1s_raw[:16, :].bitcast(I32), in_=w1_scales[0].bitcast(I32))
         nc.sync.dma_start(out=w1w_raw[:], in_=as_words(w1_words))
         load_scale_rows(nc.sync, xs, x_scales, [0, 2, 1, 3])
         nc.sync.dma_start(out=xw[:], in_=as_words(x_words))
         nc.scalar.activation(warm[:], warm_in[:], ACT.Tanh)
-        load_scale_rows(nc.sync, w1s_raw, w1_scales, [1, 2, 3])
-        nc.sync.dma_start(out=w2w_raw[:], in_=as_words(w2_words))
         nc.sync.dma_start(la_t[:], la)
+        nc.vector.tensor_copy(out=w1s[:].rearrange("p (t g i) -> p g t i", t=PACK, i=16),
+                              in_=w1s_raw[:].rearrange("p (g i t) -> p g t i", t=PACK, i=16))
+        for q in (1, 2, 3):
+            nc.sync.dma_start(out=w1s[32 * q : 32 * q + 4, :].bitcast(I32), in_=w1s[4 * q : 4 * q + 4, :].bitcast(I32))
+        nc.sync.dma_start(out=w2w_raw[:], in_=as_words(w2_words))
         load_scale_rows(nc.sync, w2s_raw, w2_scales, [0, 1])
         nc.sync.dma_start(lb_t[:], lb)
         load_scale_rows(nc.sync, w2s_raw, w2_scales, [2, 3])
@@ -86,10 +89,6 @@ def tile_picked_fixedpt_tanh_po_kernel(tc, x_words, x_scales, w1_words, w1_scale
         halves = [slice(0, HALF), slice(HALF, S)]
         xgw = [keep.tile([P, HALF], I32, name="xgw0", align_bytes=64)]
         nc.vector.tensor_copy(xgw[0][:].bitcast(U32), xw[:].bitcast(U32).indirect(offs_t[:, : HALF // 16]))
-        dealt_planes = w1s[:].rearrange("p (t m) -> p t m", t=PACK)
-        raw_planes = w1s_raw[:].rearrange("p (m t) -> p t m", t=PACK)
-        for planes in (slice(0, 1), slice(2, 3), slice(1, 4, 2)):
-            nc.gpsimd.tensor_copy(out=dealt_planes[:, planes, :], in_=raw_planes[:, planes, :])
         xgw.append(keep.tile([P, HALF], I32, name="xgw1", align_bytes=64))
         for first in (0, CHUNK):
             nc.vector.tensor_copy(xgw[1][:, first : first + CHUNK].bitcast(U32),

@@ -46,14 +46,14 @@ def tile_picked_fixedpt_tanh_po_kernel(tc, x_words, x_scales, w1_words, w1_scale
         offs_t = keep.tile([P, S // 16], U16, name="offs_t")
         la_t = keep.tile([P, V // 16], U16, name="la_t")
         lb_t = keep.tile([P, V // 16], U16, name="lb_t")
-        xw = keep.tile([P, T], I32, name="xw", tag="xw_slot", align_bytes=64)
-        xs = keep.tile([P, T], U8, name="xs", tag="xs_slot", align_bytes=64)
-        w1w_raw = keep.tile([P, H], I32, name="w1w_raw", tag="w1w_slot", align_bytes=64)
-        w1s_raw = keep.tile([P, H], U8, name="w1s_raw", tag="w1s_slot", align_bytes=64)
+        xw = keep.tile([P, T], I32, name="xw", tag="xw_slot", align_bytes=256)
+        xs = keep.tile([P, T], U8, name="xs", tag="xs_slot", align_bytes=256)
+        w1w_raw = keep.tile([P, H], I32, name="w1w_raw", tag="w1w_slot", align_bytes=256)
+        w1s_raw = keep.tile([P, H], U8, name="w1s_raw", tag="w1s_slot", align_bytes=256)
         w1w = keep.tile([P, H], I32, name="w1w", align_bytes=64)
-        w1s = keep.tile([P, H], U8, name="w1s", align_bytes=64)
-        w2w_raw = keep.tile([P, N], I32, name="w2w_raw", align_bytes=64)
-        w2s_raw = keep.tile([P, N], U8, name="w2s_raw", align_bytes=64)
+        w1s = keep.tile([P, H], U8, name="w1s", align_bytes=256)
+        w2w_raw = keep.tile([P, N], I32, name="w2w_raw", align_bytes=256)
+        w2s_raw = keep.tile([P, N], U8, name="w2s_raw", align_bytes=256)
         gain = keep.tile([P, PACK], F32, name="gain", align_bytes=64)
         warm_in = keep.tile([P, 1], F32, name="warm_in")
         warm = keep.tile([P, 1], F32, name="warm")
@@ -216,8 +216,8 @@ def tile_picked_fixedpt_tanh_po_kernel(tc, x_words, x_scales, w1_words, w1_scale
 
         zw = keep.tile([P, S], I32, name="zw", align_bytes=64)
         zs = keep.tile([P, S], U8, name="zs", align_bytes=64)
-        ow = keep.tile([P, S], I32, name="ow", align_bytes=64)
-        osc = keep.tile([P, S], U8, name="osc", align_bytes=64)
+        ow = keep.tile([P, S], I32, name="ow", align_bytes=256)
+        osc = keep.tile([P, S], U8, name="osc", align_bytes=256)
         out_rows = out_0.rearrange("(p t) j -> p t j", t=PACK)
         out_words = as_words(out_1)
         res = []
@@ -228,7 +228,7 @@ def tile_picked_fixedpt_tanh_po_kernel(tc, x_words, x_scales, w1_words, w1_scale
         pairs = [range(0, 2), range(2, PACK)]
         for c in range(CHUNKS):
             cols = slice(c * CHUNK, (c + 1) * CHUNK)
-            o_sb = keep.tile([P, PACK, CHUNK], F32, name="o_sb%d" % c, align_bytes=64)
+            o_sb = keep.tile([P, PACK, CHUNK], F32, name="o_sb%d" % c, align_bytes=256)
             groups = pairs if c < CHUNKS - 1 else [pairs[0], range(2, 3), range(3, PACK)]
             for g, planes in enumerate(groups):
                 o_ps = psum.tile([P, len(planes), CHUNK], F32, name=bank_names[(2 * c + g) % len(bank_names)])

from contextlib import ExitStack

import concourse.mybir as mybir

K, T, S, V, H, N = 512, 2048, 512, 256, 512, 512
FLOPS = 2 * K * H * S + 2 * H * N * S

F32 = mybir.dt.float32
BF16 = mybir.dt.bfloat16
I32 = mybir.dt.int32
U32 = mybir.dt.uint32
U16 = mybir.dt.uint16
U8 = mybir.dt.uint8
FP8X4 = mybir.dt.float8_e4m3fn_x4
ACT = mybir.ActivationFunctionType
ALU = mybir.AluOpType

P = 128
PACK = 4
CHUNK = 128
CHUNKS = S // CHUNK
PLANE_ORDER = (0, 2, 3, 1)


def as_words(dram):
    return dram[0].rearrange("p n t -> p (n t)").bitcast(I32)


def load_scale_rows(queue, tile, dram, quadrants):
    rows = dram[0].bitcast(I32)
    for q in quadrants:
        queue.dma_start(out=tile[32 * q : 32 * q + 4, :].bitcast(I32), in_=rows[4 * q : 4 * q + 4, :])


def deal(nc, dealt, raw):
    nc.vector.tensor_copy(out=dealt[:].rearrange("p (t m) -> p m t", t=PACK), in_=raw[:].rearrange("p (m t) -> p m t", t=PACK))


def tile_picked_fixedpt_tanh_po_kernel(tc, x_words, x_scales, w1_words, w1_scales, gn, w2_words, w2_scales, offs, la, lb, out_0, out_1, out_2):
    nc = tc.nc
    with ExitStack() as ctx:
        keep = ctx.enter_context(tc.tile_pool(name="keep", bufs=1))
        row = ctx.enter_context(tc.tile_pool(name="row", bufs=1))
        psum = ctx.enter_context(tc.psum_pool(name="psum", bufs=1))

        offs_t = keep.tile([P, S // 16], U16, name="offs_t")
        la_t = keep.tile([P, V // 16], U16, name="la_t")
        lb_t = keep.tile([P, V // 16], U16, name="lb_t")
        xw = keep.tile([P, T], I32, name="xw", tag="xw_slot", align_bytes=256)
        xs = keep.tile([P, T], U8, name="xs", tag="xs_slot", align_bytes=256)
        w1w_raw = keep.tile([P, H], I32, name="w1w_raw", tag="w1w_slot", align_bytes=256)
        w1s_raw = keep.tile([P, H], U8, name="w1s_raw", tag="w1s_slot", align_bytes=256)
        w1w = keep.tile([P, H], I32, name="w1w", align_bytes=64)
        w1s = keep.tile([P, H], U8, name="w1s", align_bytes=256)
        w2w_raw = keep.tile([P, N], I32, name="w2w_raw", align_bytes=256)
        w2s_raw = keep.tile([P, N], U8, name="w2s_raw", align_bytes=256)
        gain = keep.tile([P, PACK], F32, name="gain", align_bytes=64)
        warm_in = keep.tile([P, 1], F32, name="warm_in")
        warm = keep.tile([P, 1], F32, name="warm")
        minus_one = keep.tile([P, V], F32, name="minus_one", align_bytes=64)
        xgs = keep.tile([P, S], U8, name="xgs", align_bytes=64)

        nc.gpsimd.memset(w1s_raw[:].bitcast(I32), 0)
        nc.vector.memset(xs[:].bitcast(I32), 0)
        nc.vector.memset(warm_in[:], 0.0)
        nc.vector.memset(w2s_raw[:].bitcast(I32), 0)
        nc.vector.memset(minus_one[:], -1.0)

        nc.sync.dma_start(offs_t[:], offs)
        nc.scalar.dma_start(out=w1s_raw[:16, :].bitcast(I32), in_=w1_scales[0].bitcast(I32))
        nc.sync.dma_start(out=w1w_raw[:], in_=as_words(w1_words))
        load_scale_rows(nc.sync, xs, x_scales, [0, 2, 1, 3])
        nc.sync.dma_start(out=xw[:], in_=as_words(x_words))
        nc.scalar.activation(warm[:], warm_in[:], ACT.Tanh)
        nc.sync.dma_start(la_t[:], la)
        nc.vector.tensor_copy(out=w1s[:].rearrange("p (t g i) -> p g t i", t=PACK, i=16),
                              in_=w1s_raw[:].rearrange("p (g i t) -> p g t i", t=PACK, i=16))
        for q in (1, 2, 3):
            nc.sync.dma_start(out=w1s[32 * q : 32 * q + 4, :].bitcast(I32), in_=w1s[4 * q : 4 * q + 4, :].bitcast(I32))
        nc.sync.dma_start(out=w2w_raw[:], in_=as_words(w2_words))
        load_scale_rows(nc.sync, w2s_raw, w2_scales, [0, 1])
        nc.sync.dma_start(lb_t[:], lb)
        load_scale_rows(nc.sync, w2s_raw, w2_scales, [2, 3])
        nc.sync.dma_start(out=gain[:], in_=gn.rearrange("(p t) o -> p (t o)", t=PACK))

        deal(nc, w1w, w1w_raw)
        nc.vector.tensor_copy(xgs[:], xs[:].indirect(offs_t[:]))
        HALF = S // 2
        halves = [slice(0, HALF), slice(HALF, S)]
        xgw = [keep.tile([P, HALF], I32, name="xgw0", align_bytes=64)]
        nc.vector.tensor_copy(xgw[0][:].bitcast(U32), xw[:].bitcast(U32).indirect(offs_t[:, : HALF // 16]))
        xgw.append(keep.tile([P, HALF], I32, name="xgw1", align_bytes=64))
        for first in (0, CHUNK):
            nc.vector.tensor_copy(xgw[1][:, first : first + CHUNK].bitcast(U32),
                                  xw[:].bitcast(U32).indirect(offs_t[:, (HALF + first) // 16 : (HALF + first + CHUNK) // 16]))

        def first_product(out, t, part):
            u = part.start // HALF
            cols = slice(t * P, (t + 1) * P)
            nc.tensor.matmul_mx(out=out, lhsT=w1w[:, cols].bitcast(FP8X4), lhsT_scale=w1s[:, cols],
                                rhs=xgw[u][:, part.start - u * HALF : part.stop - u * HALF].bitcast(FP8X4), rhs_scale=xgs[:, part],
                                start=True, stop=True)

        y_ps = {}
        for t in PLANE_ORDER:
            if t == PLANE_ORDER[0]:
                y_ps[t] = []
                for n, part in enumerate([halves[0], slice(HALF, HALF + CHUNK), slice(HALF + CHUNK, S)]):
                    bank = psum.tile([P, part.stop - part.start], F32, name="y_ps%d_%d" % (t, n))
                    first_product(bank[:], t, part)
                    y_ps[t].append((part, bank))
            else:
                bank = psum.tile([P, S], F32, name="y_ps%d_0" % t)
                y_ps[t] = [(slice(0, S), bank)]
                for half in halves[::-1]:
                    first_product(bank[:, half], t, half)

        def placed(name, width, dtype, offset):
            return row.tile([P, width], dtype, name=name, offset=offset, align_bytes=64)

        def narrow(name):
            return keep.tile([P, V], F32, name=name, align_bytes=64)

        def out_of_psum(into, t, func, scale):
            for part, bank in y_ps[t]:
                nc.scalar.activation(into[:, part], bank[:], func, scale=scale)

        def look_up(into, window, lists):
            nc.scalar.activation(into[:], window[:].indirect(lists[:]), ACT.Copy)

        state = {t: keep.tile([P, S], F32, name="state%d" % t, align_bytes=64) for t in PLANE_ORDER}
        neg_p = {t: narrow("neg_p%d" % t) for t in PLANE_ORDER[:-1]}

        def put_p(t):
            nc.vector.tensor_tensor(state[t][:].indirect(la_t[:]), neg_p[t][:], minus_one[:], ALU.mult)

        def put_q(t, y_lb):
            nc.vector.tensor_tensor(state[t][:].indirect(lb_t[:]), y_lb[:], neg_p[t][:], ALU.add)

        w2w, w2s = {}, {}

        def deal_words(t, offset):
            w2w[t] = placed("w2w%d" % t, P, I32, offset)
            nc.vector.tensor_copy(out=w2w[t][:], in_=w2w_raw[:, t::PACK])

        def deal_scales(t, offset):
            w2s[t] = placed("w2s%d" % t, P, U8, offset)
            nc.vector.tensor_copy(out=w2s[t][:], in_=w2s_raw[:, t::PACK])

        a, b, c3, d = PLANE_ORDER
        R3, R4, R5, R1, R2, R6 = 0, 4352, 5888, 7424, 9408, 15552
        deal_words(0, R6)
        tanh_a = placed("tanh_a", S, F32, R1)
        out_of_psum(tanh_a, a, ACT.Tanh, -1.0)
        nc.vector.tensor_copy(neg_p[a][:, : V // 2], tanh_a[:].indirect(la_t[:, : V // 32]))
        nc.scalar.activation(neg_p[a][:, V // 2 :], tanh_a[:].indirect(la_t[:, V // 32 :]), ACT.Copy)
        put_p(a)
        deal_words(1, R1)
        tanh_b = placed("tanh_b", S, F32, R2)
        out_of_psum(tanh_b, b, ACT.Tanh, -1.0)
        y_a = placed("y_a", S, F32, R3)
        out_of_psum(y_a, a, ACT.Copy, 1.0)
        look_up(neg_p[b], tanh_b, la_t)
        put_p(b)
        deal_words(2, R2)
        ylb_a = narrow("ylb_a")
        look_up(ylb_a, y_a, lb_t)
        put_q(a, ylb_a)
        deal_words(3, R3)
        y_c = placed("y_c", S, F32, R2 + 512)
        out_of_psum(y_c, c3, ACT.Copy, 1.0)
        y_b = placed("y_b", S, F32, R3 + 512)
        out_of_psum(y_b, b, ACT.Copy, 1.0)
        yla_c = placed("yla_c", V, F32, R4)
        look_up(yla_c, y_c, la_t)
        nc.scalar.activation(neg_p[c3][:], yla_c[:], ACT.Tanh, scale=-1.0)
        put_p(c3)
        deal_scales(0, R4 + 256)
        ylb_b = placed("ylb_b", V, F32, R4 + 512)
        look_up(ylb_b, y_b, lb_t)
        put_q(b, ylb_b)
        deal_scales(1, R3 + 1536)
        y_d = placed("y_d", S, F32, R4 + 256 - 2048)
        out_of_psum(y_d, d, ACT.Copy, 1.0)
        yla_d = placed("yla_d", V, F32, R5)
        look_up(yla_d, y_d, la_t)
        neg_p[d] = placed("neg_p_last", V, F32, R3 + 512)
        nc.scalar.activation(neg_p[d][:], yla_d[:], ACT.Tanh, scale=-1.0)
        put_p(d)
        deal_scales(2, R5)
        ylb_c = placed("ylb_c", V, F32, R5 + 512)
        look_up(ylb_c, y_c, lb_t)
        put_q(c3, ylb_c)
        deal_scales(3, R2 + 1536)
        ylb_d = placed("ylb_d", V, F32, R2 + 512)
        look_up(ylb_d, y_d, lb_t)
        put_q(d, ylb_d)

        zb = row.tile([P, S, PACK], BF16, name="zb", offset=R2 + 2048, align_bytes=64)

        def round_scalar(t, cols):
            nc.scalar.activation(zb[:, cols, t], state[t][:, cols], ACT.Copy, scale=gain[:, t : t + 1])

        round_scalar(a, slice(0, S))
        gain_last = keep.tile([P, 1], F32, name="gain_last", tag="state%d" % a, align_bytes=64)
        nc.scalar.copy(gain_last[:], gain[:, d : d + 1])
        round_scalar(b, slice(0, S))
        for half in halves:
            round_scalar(c3, half)
        for c in range(CHUNKS):
            cols = slice(c * CHUNK, (c + 1) * CHUNK)
            if c < 2:
                nc.vector.tensor_scalar(zb[:, cols, d], state[d][:, cols], gain_last[:], None, ALU.mult)
            else:
                round_scalar(d, cols)

        zw = keep.tile([P, S], I32, name="zw", align_bytes=64)
        zs = keep.tile([P, S], U8, name="zs", align_bytes=64)
        ow = keep.tile([P, S], I32, name="ow", align_bytes=256)
        osc = keep.tile([P, S], U8, name="osc", align_bytes=256)
        out_rows = out_0.rearrange("(p t) j -> p t j", t=PACK)
        out_words = as_words(out_1)
        res = []
        for c in range(CHUNKS):
            cols = slice(c * CHUNK, (c + 1) * CHUNK)
            nc.vector.quantize_mx(out=zw[:, cols].bitcast(FP8X4), scales=zs[:, cols], in_=zb[:, cols, :].rearrange("p j t -> p (j t)"))
        bank_names = ["o_ps0", "o_ps1", "y_ps0_0", "y_ps0_1", "y_ps0_2", "y_ps2_0", "y_ps3_0", "y_ps1_0"]
        pairs = [range(0, 2), range(2, PACK)]
        for c in range(CHUNKS):
            cols = slice(c * CHUNK, (c + 1) * CHUNK)
            o_sb = keep.tile([P, PACK, CHUNK], F32, name="o_sb%d" % c, align_bytes=256)
            groups = pairs if c < CHUNKS - 1 else [pairs[0], range(2, 3), range(3, PACK)]
            for g, planes in enumerate(groups):
                o_ps = psum.tile([P, len(planes), CHUNK], F32, name=bank_names[(2 * c + g) % len(bank_names)])
                for t in planes:
                    nc.tensor.matmul_mx(out=o_ps[:, t - planes.start, :], lhsT=w2w[t][:].bitcast(FP8X4), lhsT_scale=w2s[t][:],
                                        rhs=zw[:, cols].bitcast(FP8X4), rhs_scale=zs[:, cols], start=True, stop=True)
                nc.scalar.copy(o_sb[:, planes.start : planes.stop, :], o_ps[:])
                if c == 0:
                    nc.sync.dma_start(out=out_rows[:, planes.start : planes.stop, cols], in_=o_sb[:, planes.start : planes.stop, :])
            if c > 0:
                nc.sync.dma_start(out=out_rows[:, :, cols], in_=o_sb[:])
            res.append((o_sb, pairs if c == CHUNKS - 1 else [range(PACK)]))
        o_bf = [keep.tile([P, CHUNK, PACK], BF16, name="o_bf%d" % c, align_bytes=64) for c in range(CHUNKS)]

        def weave(c):
            o_sb, groups = res[c]
            for planes in groups:
                part = slice(planes.start, planes.stop)
                nc.vector.tensor_copy(out=o_bf[c][:, :, part].rearrange("p (g i) t -> p g t i", i=4),
                                      in_=o_sb[:, part, :].rearrange("p t (g i) -> p g t i", i=4))

        def quantise_out(c):
            cols = slice(c * CHUNK, (c + 1) * CHUNK)
            nc.vector.quantize_mx(out=ow[:, cols].bitcast(FP8X4), scales=osc[:, cols], in_=o_bf[c][:].rearrange("p j t -> p (j t)"))

        for first in range(0, CHUNKS, 2):
            weave(first)
            weave(first + 1)
            quantise_out(first)
            quantise_out(first + 1)
        early, last = halves
        nc.sync.dma_start(out=out_words[:, early], in_=ow[:, early])
        nc.sync.dma_start(out=out_words[:, last], in_=ow[:, last])
        scale_rows = out_2[0].bitcast(I32)
        for q, queue in enumerate([nc.scalar, nc.scalar, nc.scalar, nc.sync]):
            queue.dma_start(out=scale_rows[4 * q : 4 * q + 4, :], in_=osc[32 * q : 32 * q + 4, :].bitcast(I32))
